import numpy as np
import ml_dtypes


def mxq(x, axis, fmt="e4m3"):
    dtype, down = {"e4m3": (ml_dtypes.float8_e4m3fn, 7), "e5m2": (ml_dtypes.float8_e5m2, 14)}[fmt]
    v = np.moveaxis(np.asarray(x, np.float32).astype(ml_dtypes.bfloat16).astype(np.float64), axis, -1)
    blocks = v.reshape(v.shape[:-1] + (-1, 32))
    amax = np.abs(blocks).max(-1, keepdims=True)
    byte = np.maximum(np.where(amax > 0, np.frexp(amax)[1] - 1 + 127, 0) - down, 1)
    scale = np.exp2(byte - 127.0)
    codes = (blocks / scale).astype(np.float32).astype(dtype).astype(np.float64)
    return np.moveaxis((codes * scale).reshape(v.shape), -1, axis)


WIDE = False


def mx_kscale(k):
    if not WIDE:
        return np.ones(k)
    levels = np.array([10, -10, 5, -5, 0])
    if k % 512:
        return np.exp2(np.random.permutation(np.resize(levels, k // 32))).repeat(32)
    a = np.empty((k // 512, 16))
    for p in range(k // 512):
        a[p, :8] = np.random.permutation(np.resize(levels, 8))
        for g in range(8):
            far = levels[np.abs(levels - a[p, g]) >= 10]
            a[p, g + 8] = far[np.random.randint(len(far))]
    return np.exp2(a.ravel()).repeat(32)


BF16 = ml_dtypes.bfloat16


def bf(x):
    return np.asarray(x, np.float32).astype(BF16)


def f64(x):
    return np.asarray(x).astype(np.float64)


T, S, D, C, F = 2048, 512, 1024, 1024, 512
TAU = 0.75


def sigmoid(z):
    return 1.0 / (1.0 + np.exp(-z))


def draw0():
    s, r, t = mx_kscale(D), mx_kscale(C), mx_kscale(T)
    shared = 0.5 * np.random.standard_normal((1, D))
    return {"a": bf(np.random.standard_normal((T, D)) * s),
            "c": bf(np.random.standard_normal((T, C)) * r / t[:, None]),
            "e": bf((np.random.standard_normal((S, D)) + shared) / np.sqrt(D) / s),
            "wg": bf(np.random.standard_normal((D, F)) / np.sqrt(D) / s[:, None]),
            "wv": bf(np.random.standard_normal((C, F)) / np.sqrt(C) / r[:, None]),
            "beta": bf(1.0 + 0.1 * np.random.standard_normal(S)),
            "mass": bf((1.0 + 0.1 * np.random.standard_normal(T)) * t),
            "bg": bf(0.3 * np.random.standard_normal(F)),
            "bo": bf(0.3 * np.random.standard_normal(F))}


def core(a, c, e, wg, wv, beta, mass, bg, bo):
    aq = mxq(f64(a), 1, "e4m3")
    z = (mxq(f64(e), 1, "e4m3") @ aq.T) * f64(beta)[:, None]
    p = np.exp(z - z.max(axis=1, keepdims=True))
    p = p / p.mean(axis=1, keepdims=True)
    p = p / p.mean(axis=0, keepdims=True) ** TAU
    p = p / p.mean(axis=1, keepdims=True)
    p = p * f64(mass)[None, :]
    g = sigmoid((aq @ mxq(f64(wg), 0, "e4m3")) + f64(bg))
    v = (mxq(f64(c), 1, "e4m3") @ mxq(f64(wv), 0, "e4m3")) * g
    y = mxq(p, 1, "e4m3") @ mxq(v, 0, "e4m3")
    return y / np.sqrt(T) + f64(bo)


def e4m3fn_bytes(y):
    return np.clip(np.asarray(y, np.float64), -448.0, 448.0).astype(np.float32).astype(ml_dtypes.float8_e4m3fn).view(np.uint8)


def e4m3fn_values(b):
    return np.asarray(b, np.uint8).view(ml_dtypes.float8_e4m3fn).astype(np.float64)


def setup_inputs():
    d = draw0()
    x0 = np.asarray(d['a']).astype(np.float64)
    s = (np.max(np.abs(x0), axis=(0,), keepdims=True) / 448.0).astype(np.float32)
    out = {}
    for k, v in d.items():
        if k == 'a':
            out['a_bytes'] = e4m3fn_bytes(x0 / s.astype(np.float64))
            out['a_scale'] = s
        else:
            out[k] = v
    return out


def reference(a_bytes, a_scale, c, e, wg, wv, beta, mass, bg, bo):
    return core(e4m3fn_values(a_bytes) * a_scale.astype(np.float64), c, e, wg, wv, beta, mass, bg, bo)

@@ -1,0 +1,686 @@
+from contextlib import ExitStack
+from math import sqrt
+
+import concourse.mybir as mybir
+from concourse.masks import make_identity
+
+T, S, D, C, F = 2048, 512, 1024, 1024, 512
+TAU = 0.75
+FLOPS = 2 * (S * T * D + T * D * F + T * C * F + S * T * F)
+
+F32 = mybir.dt.float32
+BF16 = mybir.dt.bfloat16
+U32 = mybir.dt.uint32
+U8 = mybir.dt.uint8
+F8 = mybir.dt.float8_e4m3fn
+FP8X4 = mybir.dt.float8_e4m3fn_x4
+ALU = mybir.AluOpType
+ACT = mybir.ActivationFunctionType
+AX = mybir.AxisListType
+
+P = 128
+CH = 4
+NT = 512
+ST = 4
+FT = 4
+KP = 2
+GB = 4
+CB = 4
+
+
+def tile_sinkhorn_slot_mixing_f5_kernel(
+    tc, a_bytes, a_scale, c, e, wg, wv, beta, mass, bg, bo, out
+):
+    nc = tc.nc
+    with ExitStack() as ctx:
+        keep = ctx.enter_context(tc.tile_pool(name="keep", bufs=1))
+        work = ctx.enter_context(tc.tile_pool(name="work", bufs=2))
+        psum = ctx.enter_context(tc.psum_pool(name="psum", bufs=4))
+
+        ident = keep.tile([P, P], F32, name="ident")
+        make_identity(nc, ident[:])
+        ident16 = keep.tile([P, P], BF16, name="ident16")
+        make_identity(nc, ident16[:])
+
+        scale = keep.tile([P, D], F32, name="scale")
+        ab = [keep.tile([P, 4, D], U8, name="ab%d" % i) for i in range(CH)]
+        e_raw = keep.tile([P, ST, D], BF16, name="e_raw")
+        vec = keep.tile([P, P], BF16, name="vec")
+        mass_n = keep.tile([P, T], BF16, name="mass_n")
+        mass_p = keep.tile([P, T], BF16, name="mass_p")
+        bo_b = keep.tile([P, F], BF16, name="bo_b")
+        a_codes = [keep.tile([P, KP, NT], U32, name="a_codes%d" % i, align_bytes=64) for i in range(CH)]
+        a_planes = [keep.tile([P, KP, NT], U8, name="a_planes%d" % i, align_bytes=64) for i in range(CH)]
+        e_codes = keep.tile([P, KP, S], U32, name="e_codes", align_bytes=64)
+        e_planes = keep.tile([P, KP, S], U8, name="e_planes", align_bytes=64)
+        wg_codes = keep.tile([P, KP, F], U32, name="wg_codes", align_bytes=64)
+        wg_planes = keep.tile([P, KP, F], U8, name="wg_planes", align_bytes=64)
+        wv_codes = keep.tile([P, KP, F], U32, name="wv_codes", align_bytes=64)
+        wv_planes = keep.tile([P, KP, F], U8, name="wv_planes", align_bytes=64)
+        v_codes = [keep.tile([P, F], U32, name="v_codes%d" % i, align_bytes=64) for i in range(CH)]
+        v_planes = [keep.tile([P, F], U8, name="v_planes%d" % i, align_bytes=64) for i in range(CH)]
+        ew = keep.tile([P, ST, T], F32, name="ew")
+        nbeta = keep.tile([P, ST], F32, name="nbeta")
+        bgh = keep.tile([P, FT], F32, name="bgh")
+        nm = keep.tile([P, ST, CH], F32, name="nm")
+        s_acc = keep.tile([P, ST, CH], F32, name="s_acc")
+        q_acc = keep.tile([P, ST, CH], F32, name="q_acc")
+        expo = keep.tile([P, 4], F32, name="expo")
+        dummy = keep.tile([P, 1], F32, name="dummy")
+
+        a_view = a_bytes.rearrange("(c m t) d -> c m t d", c=CH, m=P, t=4)
+        c_view = c.rearrange("(c m t) d -> c m t d", c=CH, m=P, t=4)
+
+        nc.vector.memset(vec[:], 0.0)
+        nc.vector.memset(dummy[:], 0.0)
+        nc.gpsimd.memset(expo[:], -TAU)
+
+        x = {}
+        grouped = {}
+        gated = {}
+        th = {}
+        c_raw = {}
+        w_raw = {}
+        banks = {}
+        codes = {}
+        pt = {}
+        small = {}
+        w_codes = {"wg": (wg_codes, wg_planes), "wv": (wv_codes, wv_planes)}
+
+        def bank(key, tag):
+            banks[key] = psum.tile([P, 512], F32, name="bank_" + tag, tag=tag, bufs=4)
+            return banks[key]
+
+        def group(key):
+            if key not in grouped:
+                grouped[key] = work.tile([P, 2048], BF16, name="grouped", tag="grouped", bufs=GB, align_bytes=64)
+            return grouped[key]
+
+        def turn(key, i, words):
+            b = bank((key, i), "tr")
+            for j in range(4):
+                nc.tensor.transpose(b[:, P * j : P * (j + 1)], words(j // 2, j % 2), ident[:])
+
+        def weave(key, i, dst, h, pattern):
+            nc.scalar.copy(
+                out=group(dst)[:].bitcast(F32)[:, 512 * h : 512 * (h + 1)].rearrange("p (a r u) -> p a r u", a=2, u=2) if pattern == 0
+                else group(dst)[:].bitcast(F32)[:, 512 * h : 512 * (h + 1)].rearrange("p (r a u) -> p r a u", a=2, u=2),
+                in_=banks[key, i][:].rearrange("p (a u r) -> p a r u", a=2, u=2) if pattern == 0
+                else banks[key, i][:].rearrange("p (a u r) -> p r a u", a=2, u=2),
+            )
+
+        def load_c(i):
+            c_raw[i] = work.tile([P, 4, C], BF16, name="c_raw", tag="c_raw", bufs=2)
+            nc.sync.dma_start(out=c_raw[i][:], in_=c_view[i])
+
+        def load_w(key, w):
+            w_raw[key] = work.tile([P, KP, 4, F], BF16, name="w_raw", tag="w_raw", bufs=1)
+            nc.sync.dma_start(out=w_raw[key][:], in_=w.rearrange("(g p j) f -> p g j f", p=P, j=4))
+
+        def prod(i, t):
+            x[i, t] = work.tile([P, D], BF16, name="x", tag="x", bufs=4)
+            nc.vector.tensor_tensor(out=x[i, t][:], in0=ab[i][:, t, :].bitcast(F8), in1=scale[:], op=ALU.mult)
+
+        def step2(words, g, u):
+            return words[:, 256 * g + u : 256 * (g + 1) : 2]
+
+        def ta(i, h, g):
+            turn("a", (i, h, g), lambda a, u: step2(x[i, 2 * h + a][:].bitcast(F32), g, u))
+
+        def ea(i, h, g):
+            weave("a", (i, h, g), ("a", i, g), h, 1)
+
+        def tc_(i, h, g):
+            turn("c", (i, h, g), lambda a, u: step2(c_raw[i][:, 2 * h + a, :].bitcast(F32), g, u))
+
+        def ec(i, h, g):
+            weave("c", (i, h, g), ("c", i, g), h, 1)
+
+        def te(g, h):
+            turn("e", (g, h), lambda a, u: step2(e_raw[:, 2 * h + a, :].bitcast(F32), g, u))
+
+        def ee(g, h):
+            weave("e", (g, h), ("e", g), h, 0)
+
+        def tv(i, h):
+            turn("tv", (i, h), lambda a, u: gated[i][:, 2 * h + a, :].bitcast(F32)[:, P * u : P * (u + 1)])
+
+        def ev(i, h):
+            weave("tv", (i, h), ("v", i), h, 0)
+
+        def tp(s, h):
+            turn("tp", (s, h), lambda a, u: pt[s][:].bitcast(F32)[:, 256 * (2 * h + a) + P * u : 256 * (2 * h + a) + P * (u + 1)])
+
+        def ep(s, h):
+            weave("tp", (s, h), ("p", s), h, 0)
+
+        def ww(key, g, h):
+            nc.scalar.copy(
+                out=group((key, g))[:, 1024 * h : 1024 * (h + 1)].rearrange("p (f j) -> p f j", j=4),
+                in_=w_raw[key][:, g, :, 256 * h : 256 * (h + 1)].rearrange("p j f -> p f j"),
+            )
+
+        def quant(dst, plane, key):
+            nc.vector.quantize_mx(out=dst.bitcast(FP8X4), scales=plane, in_=grouped[key][:])
+
+        def qa(i, g):
+            quant(a_codes[i][:, g, :], a_planes[i][:, g, :], ("a", i, g))
+
+        def qc(i, g):
+            cc = work.tile([P, NT], U32, name="c_codes", tag="c_codes", bufs=CB, align_bytes=64)
+            cp = work.tile([P, NT], U8, name="c_planes", tag="c_planes", bufs=CB, align_bytes=64)
+            codes["c", i, g] = (cc, cp)
+            quant(cc[:], cp[:], ("c", i, g))
+
+        def qe(g):
+            quant(e_codes[:, g, :], e_planes[:, g, :], ("e", g))
+
+        def qw(key, g):
+            quant(w_codes[key][0][:, g, :], w_codes[key][1][:, g, :], (key, g))
+
+        def qv(i):
+            quant(v_codes[i][:], v_planes[i][:], ("v", i))
+
+        def qp(s):
+            pc = work.tile([P, CH * P], U32, name="p_codes", tag="p_codes", bufs=4, align_bytes=64)
+            pp = work.tile([P, CH * P], U8, name="p_planes", tag="p_planes", bufs=4, align_bytes=64)
+            codes["p", s] = (pc, pp)
+            quant(pc[:], pp[:], ("p", s))
+
+        def mm(b, lhs, lhs_p, rhs, rhs_p, first, last):
+            nc.tensor.matmul_mx(out=b[:], lhsT=lhs.bitcast(FP8X4), lhsT_scale=lhs_p, rhs=rhs.bitcast(FP8X4), rhs_scale=rhs_p, start=first, stop=last)
+
+        def mz(i, s):
+            b = bank(("z", i, s), "mm")
+            for g in range(KP):
+                mm(b, e_codes[:, g, P * s : P * (s + 1)], e_planes[:, g, P * s : P * (s + 1)], a_codes[i][:, g, :], a_planes[i][:, g, :], g == 0, g == 1)
+
+        def mg(i, f):
+            b = bank(("g", i, f), "mm")
+            for g in range(KP):
+                mm(b, wg_codes[:, g, P * f : P * (f + 1)], wg_planes[:, g, P * f : P * (f + 1)], a_codes[i][:, g, :], a_planes[i][:, g, :], g == 0, g == 1)
+
+        def mv(i, f):
+            b = bank(("v", i, f), "mm")
+            for g in range(KP):
+                mm(b, wv_codes[:, g, P * f : P * (f + 1)], wv_planes[:, g, P * f : P * (f + 1)], codes["c", i, g][0][:], codes["c", i, g][1][:], g == 0, g == 1)
+
+        def chunk(i):
+            return slice(NT * i, NT * (i + 1))
+
+        def zb(i, s):
+            nc.vector.tensor_scalar(
+                out=ew[:, s, chunk(i)], in0=banks["z", i, s][:], scalar1=nbeta[:, s : s + 1], scalar2=3.0e38,
+                op0=ALU.mult, op1=ALU.min, accum_out=nm[:, s, i : i + 1],
+            )
+
+        def ex(i, s):
+            nc.scalar.activation(
+                out=ew[:, s, chunk(i)], in_=ew[:, s, chunk(i)], func=ACT.Exp, bias=nm[:, s, i : i + 1], scale=-1.0,
+                accum_out=s_acc[:, s, i : i + 1],
+            )
+
+        def tg(i, f):
+            if i not in th:
+                th[i] = work.tile([P, FT, NT], F32, name="th", tag="th", bufs=3)
+            nc.scalar.activation(out=th[i][:, f, :], in_=banks["g", i, f][:], func=ACT.Tanh, bias=bgh[:, f : f + 1], scale=0.5)
+
+        def gt(i, f):
+            if i not in gated:
+                gated[i] = work.tile([P, FT, NT], BF16, name="gated", tag="gated", bufs=2)
+            nc.vector.scalar_tensor_tensor(
+                out=gated[i][:, f, :], in0=th[i][:, f, :], scalar=1.0, in1=banks["v", i, f][:], op0=ALU.add, op1=ALU.mult
+            )
+
+        def vec_t():
+            banks["vec"] = psum.tile([P, 1024], BF16, name="bank_vec", tag="tr", bufs=4)
+            nc.tensor.transpose(banks["vec"][:, 0:P], vec[:], ident16[:])
+
+        def vec_bg():
+            nc.vector.tensor_scalar(out=bgh[:], in0=banks["vec"][:, 0:4], scalar1=0.5, scalar2=None, op0=ALU.mult)
+
+        def vec_beta():
+            nc.vector.tensor_scalar(out=nbeta[:], in0=banks["vec"][:, 4:8], scalar1=-1.0, scalar2=None, op0=ALU.mult)
+
+        def mass_order():
+            nc.scalar.copy(
+                out=mass_p[:].bitcast(F32).rearrange("q (c u p) -> q c u p", c=CH, u=2),
+                in_=mass_n[:].bitcast(F32).rearrange("q (c p u) -> q c u p", c=CH, u=2),
+            )
+
+        def wide(t):
+            return t[:].unsqueeze(2).to_broadcast([P, ST, CH])
+
+        def stat(name, shape):
+            small[name] = keep.tile(shape, F32, name=name)
+            return small[name]
+
+        def max_all():
+            nc.vector.tensor_reduce(out=stat("nmin", [P, ST])[:], in_=nm[:], axis=AX.X, op=ALU.min)
+
+        def max_diff():
+            nc.vector.tensor_tensor(out=stat("d", [P, ST, CH])[:], in0=wide(small["nmin"]), in1=nm[:], op=ALU.subtract)
+
+        def max_corr():
+            nc.scalar.activation(out=stat("corr", [P, ST, CH])[:], in_=small["d"][:], func=ACT.Exp)
+
+        def n1(tag, acc):
+            nc.vector.tensor_tensor(out=stat(tag + "_prod", [P, ST, CH])[:], in0=small["corr"][:], in1=acc[:], op=ALU.mult)
+
+        def n2(tag):
+            nc.vector.tensor_reduce(out=stat(tag + "_sum", [P, ST])[:], in_=small[tag + "_prod"][:], axis=AX.X, op=ALU.add)
+
+        def n3(tag):
+            nc.vector.reciprocal(out=stat(tag + "_rec", [P, ST])[:], in_=small[tag + "_sum"][:])
+
+        def n4(tag):
+            nc.vector.tensor_tensor(out=stat(tag, [P, ST, CH])[:], in0=small["corr"][:], in1=wide(small[tag + "_rec"]), op=ALU.mult)
+
+        def sums(i):
+            b = bank(("r", i), "tr")
+            for k in range(4):
+                for s in range(ST):
+                    nc.tensor.matmul(
+                        b[:, k : k + 1], lhsT=ew[:, s, NT * i + P * k : NT * i + P * (k + 1)], rhs=small["first"][:, s, i : i + 1],
+                        start=(s == 0), stop=(s == ST - 1),
+                    )
+
+        def pw1(i):
+            nc.vector.tensor_scalar(out=stat("rc%d" % i, [P, 4])[:], in0=banks["r", i][:, 0:4], scalar1=1.0e-30, scalar2=None, op0=ALU.max)
+
+        def pw2(i):
+            nc.gpsimd.tensor_tensor(out=stat("wt%d" % i, [P, 4])[:], in0=small["rc%d" % i][:], in1=expo[:], op=ALU.pow)
+
+        def spread(i):
+            b = bank(("w", i), "tr")
+            for k in range(4):
+                nc.tensor.transpose(b[:, P * k : P * (k + 1)], small["wt%d" % i][:, k : k + 1].to_broadcast([P, P]), ident[:])
+
+        def bal(i, s):
+            nc.vector.scalar_tensor_tensor(
+                out=ew[:, s, chunk(i)], in0=ew[:, s, chunk(i)], scalar=1.0, in1=banks["w", i][:], op0=ALU.mult, op1=ALU.mult,
+                accum_out=q_acc[:, s, i : i + 1],
+            )
+
+        def weigh(s, i):
+            if s not in pt:
+                pt[s] = work.tile([P, T], BF16, name="pt", tag="pt", bufs=2)
+            nc.vector.scalar_tensor_tensor(
+                out=pt[s][:, chunk(i)], in0=ew[:, s, chunk(i)], scalar=small["second"][:, s, i : i + 1], in1=mass_p[:, chunk(i)],
+                op0=ALU.mult, op1=ALU.mult,
+            )
+
+        def my(s):
+            b = bank(("y", s), "mm")
+            pc, pp = codes["p", s]
+            for i in range(CH):
+                cols = slice(P * i, P * (i + 1))
+                mm(b, pc[:, cols], pp[:, cols], v_codes[i][:], v_planes[i][:], i == 0, i == CH - 1)
+
+        def fin(s):
+            y = work.tile([P, F], F32, name="y", tag="y", bufs=4)
+            nc.vector.scalar_tensor_tensor(out=y[:], in0=banks["y", s][:], scalar=0.5 * sqrt(T), in1=bo_b[:], op0=ALU.mult, op1=ALU.add)
+            nc.sync.dma_start(out=out[P * s : P * (s + 1), :], in_=y[:])
+
+        ctx.enter_context(tc.manual_schedule())
+
+        nc.sync.dma_start(out=ab[0][:, 0:2, :], in_=a_view[0][:, 0:2, :])
+        nc.scalar.dma_start(out=vec[0:4, :], in_=bg.rearrange("(r f) -> r f", f=P))
+        nc.scalar.dma_start(out=vec[4:8, :], in_=beta.rearrange("(r f) -> r f", f=P))
+        nc.scalar.activation(out=dummy[:], in_=dummy[:], func=ACT.Exp)
+        nc.sync.dma_start(out=scale[:], in_=a_scale.rearrange("o k -> (o k)").partition_broadcast(P))
+        nc.sync.dma_start(out=ab[0][:, 2:4, :], in_=a_view[0][:, 2:4, :])
+        nc.sync.dma_start(out=ab[1][:], in_=a_view[1])
+        nc.sync.dma_start(out=e_raw[:], in_=e.rearrange("(s p) d -> p s d", p=P))
+        load_w("wg", wg)
+        nc.sync.dma_start(out=ab[2][:], in_=a_view[2])
+        nc.sync.dma_start(out=ab[3][:], in_=a_view[3])
+
+        prod(0, 1)
+        prod(0, 0)
+        prod(1, 2)
+        ta(0, 0, 1)
+        ta(0, 0, 0)
+        ea(0, 0, 1)
+        prod(1, 1)
+        te(1, 0)
+        ea(0, 0, 0)
+        te(1, 1)
+        prod(1, 3)
+        ee(1, 0)
+        te(0, 1)
+        ee(1, 1)
+        te(0, 0)
+        prod(1, 0)
+        ee(0, 1)
+        ta(1, 1, 1)
+        ee(0, 0)
+        ta(1, 1, 0)
+        qe(1)
+        ta(1, 0, 0)
+        qe(0)
+        ea(1, 1, 1)
+        ta(1, 0, 1)
+        prod(2, 0)
+        ea(1, 1, 0)
+        vec_t()
+        ea(1, 0, 0)
+        prod(3, 2)
+        ea(1, 0, 1)
+        qa(1, 1)
+        vec_beta()
+        prod(2, 1)
+        ww("wg", 0, 0)
+        qa(1, 0)
+        ww("wg", 0, 1)
+        ta(2, 0, 0)
+        prod(0, 3)
+        ta(2, 0, 1)
+        ea(2, 0, 0)
+        mz(1, 2)
+        qw("wg", 0)
+        mz(1, 1)
+        prod(3, 3)
+        mz(1, 3)
+        ea(2, 0, 1)
+        mz(1, 0)
+        zb(1, 1)
+        ta(3, 1, 0)
+        zb(1, 3)
+        ta(3, 1, 1)
+        ex(1, 1)
+        vec_bg()
+        prod(2, 2)
+        ex(1, 3)
+        prod(0, 2)
+        zb(1, 2)
+        ta(0, 1, 0)
+        prod(2, 3)
+        ta(0, 1, 1)
+        ex(1, 2)
+        ea(0, 1, 0)
+        prod(3, 1)
+        ea(0, 1, 1)
+        ta(2, 1, 1)
+        ta(2, 1, 0)
+        qa(0, 1)
+        ea(2, 1, 1)
+        qa(0, 0)
+        ea(3, 1, 1)
+        qa(2, 1)
+        mz(0, 0)
+        ea(3, 1, 0)
+        prod(3, 0)
+        mz(0, 2)
+        ww("wg", 1, 0)
+        mz(0, 3)
+        zb(0, 2)
+        ta(3, 0, 1)
+        ea(2, 1, 0)
+        zb(1, 0)
+        ta(3, 0, 0)
+        ex(0, 2)
+        mz(0, 1)
+        zb(0, 0)
+        ea(3, 0, 1)
+        qa(2, 0)
+        ex(0, 0)
+        zb(0, 1)
+        mz(2, 1)
+        ea(3, 0, 0)
+        mz(2, 2)
+        qa(3, 1)
+        ex(0, 1)
+        mz(2, 0)
+        zb(2, 1)
+        ex(1, 0)
+        zb(2, 2)
+        mz(2, 3)
+        ex(2, 1)
+        qa(3, 0)
+        ex(2, 2)
+        zb(2, 0)
+        mz(3, 3)
+        ww("wg", 1, 1)
+        zb(0, 3)
+        mz(3, 1)
+        zb(3, 3)
+        ex(2, 0)
+        mz(3, 0)
+        load_w("wv", wv)
+        load_c(0)
+        load_c(1)
+        nc.sync.dma_start(out=mass_n[:], in_=mass.partition_broadcast(P))
+        nc.sync.dma_start(out=bo_b[:], in_=bo.partition_broadcast(P))
+        zb(3, 1)
+        ex(0, 3)
+        mz(3, 2)
+        zb(3, 0)
+        ex(3, 3)
+        zb(3, 2)
+        ex(3, 1)
+        qw("wg", 1)
+        ex(3, 0)
+        zb(2, 3)
+        ex(3, 2)
+        mg(0, 2)
+        mg(0, 3)
+        ex(2, 3)
+        max_all()
+        max_diff()
+        mg(1, 2)
+        max_corr()
+        ww("wv", 0, 1)
+        mg(0, 0)
+        n1("first", s_acc)
+        n2("first")
+        n3("first")
+        n4("first")
+        sums(2)
+        tg(0, 3)
+        tg(1, 2)
+        ww("wv", 1, 0)
+        ww("wv", 0, 0)
+        sums(3)
+        pw1(2)
+        pw2(2)
+        ww("wv", 1, 1)
+        qw("wv", 0)
+        mass_order()
+        qw("wv", 1)
+        spread(2)
+        pw1(3)
+        sums(0)
+        pw2(3)
+        tg(0, 2)
+        bal(2, 0)
+        tg(0, 0)
+        bal(2, 2)
+        bal(2, 1)
+        bal(2, 3)
+        spread(3)
+        tc_(0, 0, 1)
+        pw1(0)
+        pw2(0)
+        bal(3, 1)
+        tc_(1, 1, 1)
+        ec(0, 0, 1)
+        bal(3, 2)
+        spread(0)
+        mg(2, 2)
+        ec(1, 1, 1)
+        bal(3, 3)
+        tc_(1, 0, 1)
+        bal(0, 1)
+        tg(2, 2)
+        sums(1)
+        bal(0, 0)
+        ec(1, 0, 1)
+        bal(0, 3)
+        bal(0, 2)
+        qc(1, 1)
+        tc_(0, 1, 1)
+        pw1(1)
+        bal(3, 0)
+        tc_(0, 0, 0)
+        pw2(1)
+        ec(0, 1, 1)
+        spread(1)
+        tc_(0, 1, 0)
+        ec(0, 0, 0)
+        qc(0, 1)
+        tc_(1, 1, 0)
+        bal(1, 2)
+        ec(0, 1, 0)
+        load_c(2)
+        tc_(1, 0, 0)
+        bal(1, 3)
+        ec(1, 1, 0)
+        mg(1, 0)
+        qc(0, 0)
+        load_c(3)
+        ec(1, 0, 0)
+        mg(2, 0)
+        bal(1, 1)
+        tg(1, 0)
+        mg(0, 1)
+        mv(0, 3)
+        tg(2, 0)
+        qc(1, 0)
+        mg(1, 1)
+        tg(0, 1)
+        bal(1, 0)
+        mv(0, 0)
+        gt(0, 3)
+        tg(1, 1)
+        mv(0, 1)
+        n1("second", q_acc)
+        gt(0, 0)
+        mv(1, 0)
+        n2("second")
+        mv(1, 1)
+        gt(0, 1)
+        mv(0, 2)
+        n3("second")
+        gt(1, 0)
+        tv(0, 0)
+        n4("second")
+        gt(1, 1)
+        tc_(2, 0, 0)
+        ev(0, 0)
+        weigh(1, 0)
+        mv(1, 2)
+        ec(2, 0, 0)
+        tv(1, 0)
+        weigh(1, 3)
+        tc_(2, 1, 0)
+        weigh(1, 2)
+        ev(1, 0)
+        tc_(2, 1, 1)
+        gt(0, 2)
+        ec(2, 1, 0)
+        tp(1, 1)
+        weigh(3, 0)
+        tv(0, 1)
+        ec(2, 1, 1)
+        mg(3, 2)
+        qc(2, 0)
+        ev(0, 1)
+        tc_(2, 0, 1)
+        weigh(1, 1)
+        ep(1, 1)
+        mg(1, 3)
+        weigh(3, 3)
+        ec(2, 0, 1)
+        mg(2, 3)
+        gt(1, 2)
+        tp(1, 0)
+        tg(1, 3)
+        qc(2, 1)
+        mg(3, 3)
+        tg(2, 3)
+        weigh(0, 2)
+        mv(1, 3)
+        ep(1, 0)
+        mv(2, 0)
+        weigh(0, 1)
+        tg(3, 3)
+        tc_(3, 0, 1)
+        gt(1, 3)
+        tg(3, 2)
+        tc_(3, 1, 1)
+        gt(2, 0)
+        ec(3, 0, 1)
+        tv(1, 1)
+        qv(0)
+        mv(2, 3)
+        ec(3, 1, 1)
+        weigh(3, 1)
+        tc_(3, 0, 0)
+        ev(1, 1)
+        qc(3, 1)
+        tp(3, 0)
+        qv(1)
+        ec(3, 0, 0)
+        tc_(3, 1, 0)
+        gt(2, 3)
+        mv(2, 2)
+        ep(3, 0)
+        mg(3, 0)
+        weigh(0, 0)
+        ec(3, 1, 0)
+        mg(2, 1)
+        gt(2, 2)
+        tg(3, 0)
+        tp(0, 0)
+        qc(3, 0)
+        mg(3, 1)
+        tg(2, 1)
+        qp(1)
+        mv(3, 2)
+        ep(0, 0)
+        weigh(0, 3)
+        mv(2, 1)
+        tg(3, 1)
+        gt(3, 2)
+        mv(3, 0)
+        tp(0, 1)
+        gt(2, 1)
+        mv(3, 3)
+        gt(3, 0)
+        ep(0, 1)
+        tv(2, 0)
+        weigh(2, 0)
+        mv(3, 1)
+        ev(2, 0)
+        gt(3, 3)
+        tv(2, 1)
+        gt(3, 1)
+        tv(3, 1)
+        ev(2, 1)
+        weigh(2, 1)
+        tv(3, 0)
+        ev(3, 1)
+        qv(2)
+        tp(2, 0)
+        ev(3, 0)
+        weigh(3, 2)
+        ep(2, 0)
+        qv(3)
+        tp(3, 1)
+        weigh(2, 3)
+        my(1)
+        ep(3, 1)
+        weigh(2, 2)
+        qp(3)
+        tp(2, 1)
+        qp(0)
+        my(3)
+        ep(2, 1)
+        fin(1)
+        my(0)
+        qp(2)
+        fin(3)
+        my(2)
+        fin(0)
+        fin(2)

@@ -264,29 +264,40 @@ def tile_sinkhorn_slot_mixing_f5_kernel(
         def max_corr():
             nc.scalar.activation(out=stat("corr", [P, ST, CH])[:], in_=small["d"][:], func=ACT.Exp)
 
-        def n1(tag, acc):
-            nc.vector.tensor_tensor(out=stat(tag + "_prod", [P, ST, CH])[:], in0=small["corr"][:], in1=acc[:], op=ALU.mult)
+        def first1():
+            nc.vector.tensor_tensor(out=stat("f_prod", [P, ST, CH])[:], in0=small["corr"][:], in1=s_acc[:], op=ALU.mult)
 
-        def n2(tag):
-            nc.vector.tensor_reduce(out=stat(tag + "_sum", [P, ST])[:], in_=small[tag + "_prod"][:], axis=AX.X, op=ALU.add)
+        def first2():
+            nc.vector.tensor_reduce(out=stat("f_sum", [P, ST])[:], in_=small["f_prod"][:], axis=AX.X, op=ALU.add)
 
-        def n3(tag):
-            nc.vector.reciprocal(out=stat(tag + "_rec", [P, ST])[:], in_=small[tag + "_sum"][:])
+        def first3():
+            nc.vector.reciprocal(out=stat("f_rec", [P, ST])[:], in_=small["f_sum"][:])
 
-        def n4(tag):
-            nc.vector.tensor_tensor(out=stat(tag, [P, ST, CH])[:], in0=small["corr"][:], in1=wide(small[tag + "_rec"]), op=ALU.mult)
+        def first4():
+            nc.vector.tensor_tensor(out=stat("first", [P, ST, CH])[:], in0=small["corr"][:], in1=wide(small["f_rec"]), op=ALU.mult)
+
+        def second1():
+            nc.vector.tensor_reduce(out=stat("s_sum", [P, ST])[:], in_=q_acc[:], axis=AX.X, op=ALU.add)
+
+        def second2():
+            nc.vector.reciprocal(out=stat("second", [P, ST])[:], in_=small["s_sum"][:])
+
+        def sc(i, s):
+            nc.scalar.activation(
+                out=ew[:, s, chunk(i)], in_=ew[:, s, chunk(i)], func=ACT.Copy, bias=1.0e-37, scale=small["first"][:, s, i : i + 1]
+            )
 
         def sums(i):
             b = bank(("r", i), "tr")
             for k in range(4):
                 for s in range(ST):
                     nc.tensor.matmul(
-                        b[:, k : k + 1], lhsT=ew[:, s, NT * i + P * k : NT * i + P * (k + 1)], rhs=small["first"][:, s, i : i + 1],
-                        start=(s == 0), stop=(s == ST - 1),
+                        b[:, P * k : P * (k + 1)], lhsT=ew[:, s, NT * i + P * k : NT * i + P * (k + 1)], rhs=ident[:],
+                        start=(s == 0), stop=(s == ST - 1), is_transpose=True,
                     )
 
         def pw1(i):
-            nc.vector.tensor_scalar(out=stat("rc%d" % i, [P, 4])[:], in0=banks["r", i][:, 0:4], scalar1=1.0e-30, scalar2=None, op0=ALU.max)
+            nc.vector.tensor_reduce(out=stat("rc%d" % i, [P, 4])[:], in_=banks["r", i][:].rearrange("p (k r) -> p k r", k=4), axis=AX.X, op=ALU.add)
 
         def pw2(i):
             nc.gpsimd.tensor_tensor(out=stat("wt%d" % i, [P, 4])[:], in0=small["rc%d" % i][:], in1=expo[:], op=ALU.pow)
@@ -302,11 +313,12 @@ def tile_sinkhorn_slot_mixing_f5_kernel(
                 accum_out=q_acc[:, s, i : i + 1],
             )
 
-        def weigh(s, i):
+        def weigh(s, h):
             if s not in pt:
                 pt[s] = work.tile([P, T], BF16, name="pt", tag="pt", bufs=2)
+            half = slice(T // 2 * h, T // 2 * (h + 1))
             nc.vector.scalar_tensor_tensor(
-                out=pt[s][:, chunk(i)], in0=ew[:, s, chunk(i)], scalar=small["second"][:, s, i : i + 1], in1=mass_p[:, chunk(i)],
+                out=pt[s][:, half], in0=ew[:, s, half], scalar=small["second"][:, s : s + 1], in1=mass_p[:, half],
                 op0=ALU.mult, op1=ALU.mult,
             )
 
@@ -336,351 +348,357 @@ def tile_sinkhorn_slot_mixing_f5_kernel(
         nc.sync.dma_start(out=ab[2][:], in_=a_view[2])
         nc.sync.dma_start(out=ab[3][:], in_=a_view[3])
 
-        prod(0, 1)
         prod(0, 0)
-        prod(1, 2)
+        prod(0, 1)
+        prod(1, 1)
         ta(0, 0, 1)
         ta(0, 0, 0)
-        ea(0, 0, 1)
-        prod(1, 1)
-        te(1, 0)
-        ea(0, 0, 0)
-        te(1, 1)
-        prod(1, 3)
-        ee(1, 0)
-        te(0, 1)
-        ee(1, 1)
-        te(0, 0)
-        prod(1, 0)
-        ee(0, 1)
-        ta(1, 1, 1)
-        ee(0, 0)
-        ta(1, 1, 0)
-        qe(1)
-        ta(1, 0, 0)
-        qe(0)
-        ea(1, 1, 1)
-        ta(1, 0, 1)
-        prod(2, 0)
-        ea(1, 1, 0)
-        vec_t()
-        ea(1, 0, 0)
-        prod(3, 2)
-        ea(1, 0, 1)
-        qa(1, 1)
-        vec_beta()
-        prod(2, 1)
-        ww("wg", 0, 0)
-        qa(1, 0)
-        ww("wg", 0, 1)
-        ta(2, 0, 0)
-        prod(0, 3)
-        ta(2, 0, 1)
-        ea(2, 0, 0)
-        mz(1, 2)
-        qw("wg", 0)
-        mz(1, 1)
-        prod(3, 3)
-        mz(1, 3)
-        ea(2, 0, 1)
-        mz(1, 0)
-        zb(1, 1)
-        ta(3, 1, 0)
-        zb(1, 3)
-        ta(3, 1, 1)
-        ex(1, 1)
-        vec_bg()
-        prod(2, 2)
-        ex(1, 3)
         prod(0, 2)
-        zb(1, 2)
-        ta(0, 1, 0)
-        prod(2, 3)
+        ea(0, 0, 1)
+        te(0, 1)
+        ea(0, 0, 0)
+        prod(0, 3)
+        te(1, 0)
+        ee(0, 1)
+        te(0, 0)
+        ee(1, 0)
+        prod(1, 2)
+        te(1, 1)
+        ee(0, 0)
         ta(0, 1, 1)
-        ex(1, 2)
-        ea(0, 1, 0)
-        prod(3, 1)
+        ee(1, 1)
+        ta(0, 1, 0)
+        qe(0)
         ea(0, 1, 1)
-        ta(2, 1, 1)
-        ta(2, 1, 0)
+        qe(1)
+        ww("wg", 0, 0)
+        prod(1, 0)
+        vec_t()
+        ww("wg", 0, 1)
+        prod(1, 3)
+        ta(1, 0, 1)
+        ta(1, 0, 0)
+        ea(0, 1, 0)
         qa(0, 1)
-        ea(2, 1, 1)
-        qa(0, 0)
-        ea(3, 1, 1)
-        qa(2, 1)
-        mz(0, 0)
-        ea(3, 1, 0)
-        prod(3, 0)
-        mz(0, 2)
-        ww("wg", 1, 0)
-        mz(0, 3)
-        zb(0, 2)
-        ta(3, 0, 1)
-        ea(2, 1, 0)
-        zb(1, 0)
-        ta(3, 0, 0)
-        ex(0, 2)
-        mz(0, 1)
-        zb(0, 0)
-        ea(3, 0, 1)
-        qa(2, 0)
-        ex(0, 0)
-        zb(0, 1)
-        mz(2, 1)
-        ea(3, 0, 0)
-        mz(2, 2)
-        qa(3, 1)
-        ex(0, 1)
-        mz(2, 0)
-        zb(2, 1)
-        ex(1, 0)
-        zb(2, 2)
-        mz(2, 3)
-        ex(2, 1)
-        qa(3, 0)
-        ex(2, 2)
-        zb(2, 0)
-        mz(3, 3)
+        ea(1, 0, 1)
+        qw("wg", 0)
+        ta(1, 1, 0)
         ww("wg", 1, 1)
-        zb(0, 3)
-        mz(3, 1)
-        zb(3, 3)
-        ex(2, 0)
-        mz(3, 0)
+        qa(0, 0)
+        ta(1, 1, 1)
+        prod(2, 2)
+        mz(0, 3)
+        ww("wg", 1, 0)
+        vec_beta()
+        prod(2, 3)
+        mz(0, 0)
+        ea(1, 1, 1)
         load_w("wv", wv)
         load_c(0)
         load_c(1)
         nc.sync.dma_start(out=mass_n[:], in_=mass.partition_broadcast(P))
         nc.sync.dma_start(out=bo_b[:], in_=bo.partition_broadcast(P))
-        zb(3, 1)
+        ea(1, 1, 0)
+        zb(0, 3)
+        ta(2, 1, 0)
+        ea(1, 0, 0)
+        qa(1, 1)
         ex(0, 3)
-        mz(3, 2)
-        zb(3, 0)
-        ex(3, 3)
-        zb(3, 2)
-        ex(3, 1)
+        ta(2, 1, 1)
+        zb(0, 0)
+        mz(0, 2)
+        ea(2, 1, 0)
+        qa(1, 0)
+        ex(0, 0)
+        mz(0, 1)
         qw("wg", 1)
-        ex(3, 0)
-        zb(2, 3)
-        ex(3, 2)
-        mg(0, 2)
+        mz(1, 0)
+        ea(2, 1, 1)
+        prod(3, 3)
         mg(0, 3)
-        ex(2, 3)
-        max_all()
-        max_diff()
-        mg(1, 2)
-        max_corr()
         ww("wv", 0, 1)
-        mg(0, 0)
-        n1("first", s_acc)
-        n2("first")
-        n3("first")
-        n4("first")
-        sums(2)
-        tg(0, 3)
-        tg(1, 2)
-        ww("wv", 1, 0)
-        ww("wv", 0, 0)
-        sums(3)
-        pw1(2)
-        pw2(2)
+        zb(0, 1)
+        zb(1, 0)
         ww("wv", 1, 1)
-        qw("wv", 0)
-        mass_order()
-        qw("wv", 1)
-        spread(2)
-        pw1(3)
-        sums(0)
-        pw2(3)
-        tg(0, 2)
-        bal(2, 0)
-        tg(0, 0)
-        bal(2, 2)
-        bal(2, 1)
-        bal(2, 3)
-        spread(3)
-        tc_(0, 0, 1)
-        pw1(0)
-        pw2(0)
-        bal(3, 1)
-        tc_(1, 1, 1)
-        ec(0, 0, 1)
-        bal(3, 2)
-        spread(0)
-        mg(2, 2)
-        ec(1, 1, 1)
-        bal(3, 3)
-        tc_(1, 0, 1)
-        bal(0, 1)
-        tg(2, 2)
-        sums(1)
-        bal(0, 0)
-        ec(1, 0, 1)
-        bal(0, 3)
-        bal(0, 2)
-        qc(1, 1)
-        tc_(0, 1, 1)
-        pw1(1)
-        bal(3, 0)
-        tc_(0, 0, 0)
-        pw2(1)
-        ec(0, 1, 1)
-        spread(1)
+        mg(0, 0)
+        prod(2, 0)
+        mg(0, 1)
+        ex(1, 0)
         tc_(0, 1, 0)
-        ec(0, 0, 0)
+        prod(3, 0)
+        ww("wv", 0, 0)
+        tc_(0, 1, 1)
+        tc_(0, 0, 1)
+        zb(0, 2)
+        ww("wv", 1, 0)
+        qw("wv", 0)
+        mg(1, 3)
+        ex(0, 2)
+        prod(3, 1)
+        ec(0, 1, 1)
+        qw("wv", 1)
+        ec(0, 0, 1)
+        ta(3, 0, 0)
+        ex(0, 1)
+        vec_bg()
         qc(0, 1)
-        tc_(1, 1, 0)
-        bal(1, 2)
-        ec(0, 1, 0)
+        ta(3, 0, 1)
+        tg(1, 3)
+        tc_(1, 0, 1)
+        ea(3, 0, 0)
+        prod(3, 2)
+        mg(0, 2)
+        tg(0, 3)
+        tc_(0, 0, 0)
+        tg(0, 0)
+        prod(2, 1)
+        mg(1, 2)
+        tg(0, 2)
         load_c(2)
-        tc_(1, 0, 0)
-        bal(1, 3)
-        ec(1, 1, 0)
+        ec(0, 0, 0)
+        mz(1, 2)
+        mz(1, 3)
+        tg(1, 2)
+        zb(1, 2)
+        ta(3, 1, 0)
+        ec(0, 1, 0)
+        zb(1, 3)
+        mass_order()
         mg(1, 0)
         qc(0, 0)
+        ta(2, 0, 0)
+        ea(3, 1, 0)
+        mv(0, 2)
+        ex(1, 2)
+        qa(3, 0)
+        ta(2, 0, 1)
+        tg(0, 1)
+        gt(0, 2)
+        mz(1, 1)
+        ea(2, 0, 0)
+        mv(0, 1)
+        ea(2, 0, 1)
+        qa(2, 0)
+        tc_(1, 1, 1)
+        ea(3, 0, 1)
+        zb(1, 1)
+        tg(1, 0)
+        tc_(1, 1, 0)
+        gt(0, 1)
+        ex(1, 1)
+        mv(0, 0)
+        qa(2, 1)
+        ec(1, 1, 0)
+        ta(3, 1, 1)
+        gt(0, 0)
+        ec(1, 1, 1)
+        mz(2, 1)
+        ex(1, 3)
+        mz(2, 2)
+        ea(3, 1, 1)
+        zb(2, 1)
+        mz(2, 0)
+        ec(1, 0, 1)
+        zb(2, 2)
+        mz(2, 3)
+        ex(2, 1)
+        tv(0, 0)
+        qa(3, 1)
+        ex(2, 2)
+        mg(2, 2)
+        zb(2, 3)
+        ev(0, 0)
+        mz(3, 0)
+        zb(2, 0)
+        ex(2, 3)
+        mz(3, 1)
+        qc(1, 1)
+        ex(2, 0)
+        mz(3, 3)
+        zb(3, 0)
+        tg(2, 2)
+        tc_(1, 0, 0)
+        zb(3, 1)
+        ex(3, 0)
+        mz(3, 2)
+        zb(3, 3)
         load_c(3)
         ec(1, 0, 0)
-        mg(2, 0)
-        bal(1, 1)
-        tg(1, 0)
-        mg(0, 1)
-        mv(0, 3)
-        tg(2, 0)
-        qc(1, 0)
-        mg(1, 1)
-        tg(0, 1)
-        bal(1, 0)
-        mv(0, 0)
-        gt(0, 3)
-        tg(1, 1)
-        mv(0, 1)
-        n1("second", q_acc)
-        gt(0, 0)
-        mv(1, 0)
-        n2("second")
-        mv(1, 1)
-        gt(0, 1)
-        mv(0, 2)
-        n3("second")
-        gt(1, 0)
-        tv(0, 0)
-        n4("second")
-        gt(1, 1)
-        tc_(2, 0, 0)
-        ev(0, 0)
-        weigh(1, 0)
-        mv(1, 2)
-        ec(2, 0, 0)
-        tv(1, 0)
-        weigh(1, 3)
-        tc_(2, 1, 0)
-        weigh(1, 2)
-        ev(1, 0)
-        tc_(2, 1, 1)
-        gt(0, 2)
-        ec(2, 1, 0)
-        tp(1, 1)
-        weigh(3, 0)
-        tv(0, 1)
-        ec(2, 1, 1)
-        mg(3, 2)
-        qc(2, 0)
-        ev(0, 1)
-        tc_(2, 0, 1)
-        weigh(1, 1)
-        ep(1, 1)
-        mg(1, 3)
-        weigh(3, 3)
-        ec(2, 0, 1)
         mg(2, 3)
-        gt(1, 2)
-        tp(1, 0)
-        tg(1, 3)
-        qc(2, 1)
-        mg(3, 3)
+        ex(3, 1)
+        zb(3, 2)
+        mv(0, 3)
+        ex(3, 3)
+        qc(1, 0)
+        tc_(2, 0, 1)
+        ex(3, 2)
+        max_all()
+        gt(0, 3)
+        tc_(2, 1, 0)
+        ec(2, 0, 1)
+        max_diff()
+        mv(1, 0)
+        max_corr()
         tg(2, 3)
-        weigh(0, 2)
-        mv(1, 3)
-        ep(1, 0)
-        mv(2, 0)
-        weigh(0, 1)
-        tg(3, 3)
-        tc_(3, 0, 1)
-        gt(1, 3)
-        tg(3, 2)
-        tc_(3, 1, 1)
-        gt(2, 0)
-        ec(3, 0, 1)
-        tv(1, 1)
+        tv(0, 1)
+        first1()
+        first2()
+        ec(2, 1, 0)
+        gt(1, 0)
+        mg(3, 2)
+        ev(0, 1)
+        first3()
+        tc_(2, 1, 1)
+        first4()
+        sc(3, 3)
         qv(0)
+        mv(1, 2)
+        sc(3, 0)
+        mv(1, 3)
+        ec(2, 1, 1)
+        gt(1, 2)
+        mg(3, 3)
+        sc(3, 1)
+        gt(1, 3)
+        tc_(2, 0, 0)
+        sc(3, 2)
+        qc(2, 1)
+        tv(1, 1)
+        sc(2, 2)
+        mg(2, 0)
+        ec(2, 0, 0)
+        sums(3)
+        sc(2, 3)
+        qc(2, 0)
+        tg(2, 0)
+        sc(2, 0)
         mv(2, 3)
-        ec(3, 1, 1)
-        weigh(3, 1)
-        tc_(3, 0, 0)
-        ev(1, 1)
-        qc(3, 1)
-        tp(3, 0)
-        qv(1)
-        ec(3, 0, 0)
-        tc_(3, 1, 0)
-        gt(2, 3)
+        pw1(3)
+        sc(2, 1)
         mv(2, 2)
-        ep(3, 0)
-        mg(3, 0)
-        weigh(0, 0)
-        ec(3, 1, 0)
-        mg(2, 1)
+        gt(2, 3)
+        sc(1, 1)
+        pw2(3)
+        sums(2)
         gt(2, 2)
+        sc(1, 2)
+        sc(1, 3)
+        spread(3)
+        sc(1, 0)
+        mg(3, 0)
+        pw1(2)
+        sc(0, 2)
+        bal(3, 0)
+        sums(1)
+        sc(0, 1)
+        pw2(2)
+        bal(3, 2)
         tg(3, 0)
-        tp(0, 0)
-        qc(3, 0)
+        bal(3, 1)
+        sc(0, 3)
+        mv(2, 0)
+        sc(0, 0)
+        pw1(1)
+        spread(2)
+        ev(1, 1)
+        bal(3, 3)
+        mg(1, 1)
+        pw2(1)
+        tg(3, 2)
+        gt(2, 0)
+        sums(0)
+        tg(3, 3)
+        bal(2, 2)
+        tg(1, 1)
+        bal(2, 3)
+        spread(1)
+        bal(2, 0)
+        mv(1, 1)
+        bal(1, 2)
+        tc_(3, 0, 0)
+        bal(1, 0)
+        mg(2, 1)
+        ec(3, 0, 0)
+        pw1(0)
         mg(3, 1)
         tg(2, 1)
-        qp(1)
-        mv(3, 2)
-        ep(0, 0)
-        weigh(0, 3)
-        mv(2, 1)
+        bal(1, 1)
+        tc_(3, 1, 1)
+        pw2(0)
         tg(3, 1)
+        gt(1, 1)
+        tc_(3, 0, 1)
+        ec(3, 1, 1)
+        bal(1, 3)
+        mv(2, 1)
+        ec(3, 0, 1)
+        bal(2, 1)
+        spread(0)
+        tv(1, 0)
+        gt(2, 1)
+        tc_(3, 1, 0)
+        bal(0, 0)
+        ev(1, 0)
+        tv(2, 0)
+        bal(0, 3)
+        ec(3, 1, 0)
+        tv(2, 1)
+        ev(2, 0)
+        qc(3, 1)
+        ev(2, 1)
+        qc(3, 0)
+        bal(0, 2)
+        mv(3, 2)
+        qv(2)
+        bal(0, 1)
+        mv(3, 3)
         gt(3, 2)
         mv(3, 0)
-        tp(0, 1)
-        gt(2, 1)
-        mv(3, 3)
-        gt(3, 0)
-        ep(0, 1)
-        tv(2, 0)
-        weigh(2, 0)
-        mv(3, 1)
-        ev(2, 0)
         gt(3, 3)
-        tv(2, 1)
-        gt(3, 1)
+        mv(3, 1)
+        second1()
+        qv(1)
         tv(3, 1)
-        ev(2, 1)
-        weigh(2, 1)
-        tv(3, 0)
+        second2()
+        gt(3, 1)
         ev(3, 1)
-        qv(2)
-        tp(2, 0)
-        ev(3, 0)
-        weigh(3, 2)
-        ep(2, 0)
-        qv(3)
+        weigh(3, 0)
+        weigh(3, 1)
+        tp(3, 0)
+        weigh(0, 1)
+        ep(3, 0)
         tp(3, 1)
-        weigh(2, 3)
-        my(1)
+        gt(3, 0)
         ep(3, 1)
-        weigh(2, 2)
+        tp(0, 1)
+        weigh(1, 0)
+        tv(3, 0)
+        ep(0, 1)
         qp(3)
+        ev(3, 0)
+        tp(1, 0)
+        weigh(0, 0)
+        ep(1, 0)
+        qv(3)
+        tp(0, 0)
+        weigh(1, 1)
+        my(3)
+        ep(0, 0)
+        weigh(2, 1)
+        weigh(2, 0)
+        tp(1, 1)
         tp(2, 1)
         qp(0)
-        my(3)
-        ep(2, 1)
-        fin(1)
-        my(0)
-        qp(2)
+        ep(1, 1)
+        tp(2, 0)
         fin(3)
-        my(2)
+        ep(2, 1)
+        my(0)
+        qp(1)
+        ep(2, 0)
+        qp(2)
+        my(1)
         fin(0)
+        my(2)
+        fin(1)
         fin(2)

@@ -25,6 +25,8 @@ ST = 4
 FT = 4
 KP = 2
 GB = 4
+TR = 5
+GS = 2
 CB = 4
 
 
@@ -67,6 +69,7 @@ def tile_sinkhorn_slot_mixing_f5_kernel(
         q_acc = keep.tile([P, ST, CH], F32, name="q_acc")
         expo = keep.tile([P, 4], F32, name="expo")
         dummy = keep.tile([P, 1], F32, name="dummy")
+        junk = keep.tile([P, P], F32, name="junk")
 
         a_view = a_bytes.rearrange("(c m t) d -> c m t d", c=CH, m=P, t=4)
         c_view = c.rearrange("(c m t) d -> c m t d", c=CH, m=P, t=4)
@@ -84,11 +87,12 @@ def tile_sinkhorn_slot_mixing_f5_kernel(
         banks = {}
         codes = {}
         pt = {}
+        pcodes = {}
         small = {}
         w_codes = {"wg": (wg_codes, wg_planes), "wv": (wv_codes, wv_planes)}
 
         def bank(key, tag):
-            banks[key] = psum.tile([P, 512], F32, name="bank_" + tag, tag=tag, bufs=4)
+            banks[key] = psum.tile([P, 512], F32, name="bank_" + tag, tag=tag, bufs=TR if tag == "tr" else 8 - TR)
             return banks[key]
 
         def group(key):
@@ -109,6 +113,10 @@ def tile_sinkhorn_slot_mixing_f5_kernel(
                 else banks[key, i][:].rearrange("p (a u r) -> p r a u", a=2, u=2),
             )
 
+        def load_scale(g):
+            cols = slice(512 * g, 512 * (g + 1))
+            nc.sync.dma_start(out=scale[:, cols], in_=a_scale[:, cols].rearrange("o k -> (o k)").partition_broadcast(P))
+
         def load_c(i):
             c_raw[i] = work.tile([P, 4, C], BF16, name="c_raw", tag="c_raw", bufs=2)
             nc.sync.dma_start(out=c_raw[i][:], in_=c_view[i])
@@ -117,9 +125,11 @@ def tile_sinkhorn_slot_mixing_f5_kernel(
             w_raw[key] = work.tile([P, KP, 4, F], BF16, name="w_raw", tag="w_raw", bufs=1)
             nc.sync.dma_start(out=w_raw[key][:], in_=w.rearrange("(g p j) f -> p g j f", p=P, j=4))
 
-        def prod(i, t):
-            x[i, t] = work.tile([P, D], BF16, name="x", tag="x", bufs=4)
-            nc.vector.tensor_tensor(out=x[i, t][:], in0=ab[i][:, t, :].bitcast(F8), in1=scale[:], op=ALU.mult)
+        def prod(i, t, g=None):
+            cols = slice(0, D) if g is None else slice(D // 2 * g, D // 2 * (g + 1))
+            if (i, t) not in x:
+                x[i, t] = work.tile([P, D], BF16, name="x", tag="x", bufs=5)
+            nc.vector.tensor_tensor(out=x[i, t][:, cols], in0=ab[i][:, t, cols].bitcast(F8), in1=scale[:, cols], op=ALU.mult)
 
         def step2(words, g, u):
             return words[:, 256 * g + u : 256 * (g + 1) : 2]
@@ -181,11 +191,16 @@ def tile_sinkhorn_slot_mixing_f5_kernel(
         def qv(i):
             quant(v_codes[i][:], v_planes[i][:], ("v", i))
 
-        def qp(s):
-            pc = work.tile([P, CH * P], U32, name="p_codes", tag="p_codes", bufs=4, align_bytes=64)
-            pp = work.tile([P, CH * P], U8, name="p_planes", tag="p_planes", bufs=4, align_bytes=64)
-            codes["p", s] = (pc, pp)
-            quant(pc[:], pp[:], ("p", s))
+        def qp(s, h=None):
+            if s not in pcodes:
+                pc = work.tile([P, CH * P], U32, name="p_codes", tag="p_codes", bufs=4, align_bytes=64)
+                pp = work.tile([P, CH * P], U8, name="p_planes", tag="p_planes", bufs=4, align_bytes=64)
+                pcodes[s] = (pc, pp)
+            pc, pp = pcodes[s]
+            cols = slice(0, 512) if h is None else slice(256 * h, 256 * (h + 1))
+            nc.vector.quantize_mx(
+                out=pc[:, cols].bitcast(FP8X4), scales=pp[:, cols], in_=grouped["p", s][:, 4 * cols.start : 4 * cols.stop]
+            )
 
         def mm(b, lhs, lhs_p, rhs, rhs_p, first, last):
             nc.tensor.matmul_mx(out=b[:], lhsT=lhs.bitcast(FP8X4), lhsT_scale=lhs_p, rhs=rhs.bitcast(FP8X4), rhs_scale=rhs_p, start=first, stop=last)
@@ -233,7 +248,7 @@ def tile_sinkhorn_slot_mixing_f5_kernel(
             )
 
         def vec_t():
-            banks["vec"] = psum.tile([P, 1024], BF16, name="bank_vec", tag="tr", bufs=4)
+            banks["vec"] = psum.tile([P, 1024], BF16, name="bank_vec", tag="tr", bufs=TR)
             nc.tensor.transpose(banks["vec"][:, 0:P], vec[:], ident16[:])
 
         def vec_bg():
@@ -283,6 +298,12 @@ def tile_sinkhorn_slot_mixing_f5_kernel(
             nc.vector.reciprocal(out=stat("second", [P, ST])[:], in_=small["s_sum"][:])
 
         def sc(i, s):
+            if s >= GS:
+                nc.gpsimd.tensor_scalar(
+                    out=ew[:, s, chunk(i)], in0=ew[:, s, chunk(i)], scalar1=small["first"][:, s, i : i + 1], scalar2=1.0e-37,
+                    op0=ALU.mult, op1=ALU.add,
+                )
+                return
             nc.scalar.activation(
                 out=ew[:, s, chunk(i)], in_=ew[:, s, chunk(i)], func=ACT.Copy, bias=1.0e-37, scale=small["first"][:, s, i : i + 1]
             )
@@ -298,6 +319,13 @@ def tile_sinkhorn_slot_mixing_f5_kernel(
 
         def pw1(i):
             nc.vector.tensor_reduce(out=stat("rc%d" % i, [P, 4])[:], in_=banks["r", i][:].rearrange("p (k r) -> p k r", k=4), axis=AX.X, op=ALU.add)
+
+        def pr(i):
+            rc = stat("rc%d" % i, [P, 4])
+            for k in range(4):
+                nc.scalar.activation(
+                    out=junk[:], in_=banks["r", i][:, P * k : P * (k + 1)], func=ACT.Copy, accum_out=rc[:, k : k + 1]
+                )
 
         def pw2(i):
             nc.gpsimd.tensor_tensor(out=stat("wt%d" % i, [P, 4])[:], in0=small["rc%d" % i][:], in1=expo[:], op=ALU.pow)
@@ -322,10 +350,12 @@ def tile_sinkhorn_slot_mixing_f5_kernel(
                 op0=ALU.mult, op1=ALU.mult,
             )
 
-        def my(s):
-            b = bank(("y", s), "mm")
-            pc, pp = codes["p", s]
-            for i in range(CH):
+        def my(s, h=None):
+            if ("y", s) not in banks:
+                bank(("y", s), "mm")
+            b = banks["y", s]
+            pc, pp = pcodes[s]
+            for i in range(CH) if h is None else (2 * h, 2 * h + 1):
                 cols = slice(P * i, P * (i + 1))
                 mm(b, pc[:, cols], pp[:, cols], v_codes[i][:], v_planes[i][:], i == 0, i == CH - 1)
 
@@ -340,7 +370,8 @@ def tile_sinkhorn_slot_mixing_f5_kernel(
         nc.scalar.dma_start(out=vec[0:4, :], in_=bg.rearrange("(r f) -> r f", f=P))
         nc.scalar.dma_start(out=vec[4:8, :], in_=beta.rearrange("(r f) -> r f", f=P))
         nc.scalar.activation(out=dummy[:], in_=dummy[:], func=ACT.Exp)
-        nc.sync.dma_start(out=scale[:], in_=a_scale.rearrange("o k -> (o k)").partition_broadcast(P))
+        load_scale(0)
+        load_scale(1)
         nc.sync.dma_start(out=ab[0][:, 2:4, :], in_=a_view[0][:, 2:4, :])
         nc.sync.dma_start(out=ab[1][:], in_=a_view[1])
         nc.sync.dma_start(out=e_raw[:], in_=e.rearrange("(s p) d -> p s d", p=P))
@@ -348,357 +379,361 @@ def tile_sinkhorn_slot_mixing_f5_kernel(
         nc.sync.dma_start(out=ab[2][:], in_=a_view[2])
         nc.sync.dma_start(out=ab[3][:], in_=a_view[3])
 
-        prod(0, 0)
-        prod(0, 1)
-        prod(1, 1)
+        prod(0, 0, 0)
+        prod(0, 0, 1)
+        prod(0, 1, 1)
+        prod(0, 1, 0)
         ta(0, 0, 1)
-        ta(0, 0, 0)
-        prod(0, 2)
-        ea(0, 0, 1)
-        te(0, 1)
-        ea(0, 0, 0)
-        prod(0, 3)
-        te(1, 0)
-        ee(0, 1)
-        te(0, 0)
-        ee(1, 0)
         prod(1, 2)
+        ta(0, 0, 0)
+        ea(0, 0, 1)
+        prod(0, 2)
+        ea(0, 0, 0)
+        te(0, 1)
+        prod(0, 3)
         te(1, 1)
-        ee(0, 0)
-        ta(0, 1, 1)
+        ee(0, 1)
+        prod(1, 1)
+        te(1, 0)
         ee(1, 1)
-        ta(0, 1, 0)
-        qe(0)
-        ea(0, 1, 1)
-        qe(1)
-        ww("wg", 0, 0)
+        ta(0, 1, 1)
+        ee(1, 0)
         prod(1, 0)
-        vec_t()
-        ww("wg", 0, 1)
-        prod(1, 3)
-        ta(1, 0, 1)
-        ta(1, 0, 0)
+        ta(0, 1, 0)
+        ea(0, 1, 1)
+        te(0, 0)
+        qe(1)
         ea(0, 1, 0)
-        qa(0, 1)
-        ea(1, 0, 1)
-        qw("wg", 0)
-        ta(1, 1, 0)
-        ww("wg", 1, 1)
-        qa(0, 0)
-        ta(1, 1, 1)
-        prod(2, 2)
-        mz(0, 3)
+        ta(1, 0, 1)
+        prod(2, 0)
+        ee(0, 0)
+        ta(1, 0, 0)
         ww("wg", 1, 0)
+        vec_t()
+        qa(0, 1)
         vec_beta()
-        prod(2, 3)
-        mz(0, 0)
-        ea(1, 1, 1)
+        prod(2, 1)
+        ww("wg", 1, 1)
+        prod(1, 3)
+        ww("wg", 0, 0)
+        ta(2, 0, 1)
+        ta(2, 0, 0)
+        qw("wg", 1)
+        ww("wg", 0, 1)
+        qa(0, 0)
+        ea(2, 0, 1)
+        vec_bg()
+        qe(0)
         load_w("wv", wv)
+        ta(1, 1, 0)
         load_c(0)
         load_c(1)
         nc.sync.dma_start(out=mass_n[:], in_=mass.partition_broadcast(P))
         nc.sync.dma_start(out=bo_b[:], in_=bo.partition_broadcast(P))
-        ea(1, 1, 0)
-        zb(0, 3)
-        ta(2, 1, 0)
-        ea(1, 0, 0)
-        qa(1, 1)
-        ex(0, 3)
-        ta(2, 1, 1)
-        zb(0, 0)
-        mz(0, 2)
-        ea(2, 1, 0)
-        qa(1, 0)
-        ex(0, 0)
+        ea(1, 0, 1)
+        qw("wg", 0)
         mz(0, 1)
-        qw("wg", 1)
-        mz(1, 0)
-        ea(2, 1, 1)
-        prod(3, 3)
-        mg(0, 3)
-        ww("wv", 0, 1)
-        zb(0, 1)
-        zb(1, 0)
-        ww("wv", 1, 1)
+        ea(1, 0, 0)
+        prod(2, 3)
+        ea(1, 1, 0)
         mg(0, 0)
-        prod(2, 0)
-        mg(0, 1)
-        ex(1, 0)
-        tc_(0, 1, 0)
-        prod(3, 0)
-        ww("wv", 0, 0)
-        tc_(0, 1, 1)
-        tc_(0, 0, 1)
-        zb(0, 2)
-        ww("wv", 1, 0)
-        qw("wv", 0)
-        mg(1, 3)
-        ex(0, 2)
-        prod(3, 1)
-        ec(0, 1, 1)
-        qw("wv", 1)
-        ec(0, 0, 1)
-        ta(3, 0, 0)
-        ex(0, 1)
-        vec_bg()
-        qc(0, 1)
-        ta(3, 0, 1)
-        tg(1, 3)
-        tc_(1, 0, 1)
-        ea(3, 0, 0)
-        prod(3, 2)
-        mg(0, 2)
-        tg(0, 3)
-        tc_(0, 0, 0)
-        tg(0, 0)
-        prod(2, 1)
-        mg(1, 2)
-        tg(0, 2)
-        load_c(2)
-        ec(0, 0, 0)
-        mz(1, 2)
-        mz(1, 3)
-        tg(1, 2)
-        zb(1, 2)
-        ta(3, 1, 0)
-        ec(0, 1, 0)
-        zb(1, 3)
-        mass_order()
-        mg(1, 0)
-        qc(0, 0)
-        ta(2, 0, 0)
-        ea(3, 1, 0)
-        mv(0, 2)
-        ex(1, 2)
-        qa(3, 0)
-        ta(2, 0, 1)
-        tg(0, 1)
-        gt(0, 2)
-        mz(1, 1)
         ea(2, 0, 0)
-        mv(0, 1)
-        ea(2, 0, 1)
-        qa(2, 0)
-        tc_(1, 1, 1)
-        ea(3, 0, 1)
-        zb(1, 1)
-        tg(1, 0)
-        tc_(1, 1, 0)
-        gt(0, 1)
-        ex(1, 1)
-        mv(0, 0)
+        prod(2, 2)
+        mg(0, 1)
+        qa(1, 0)
+        tg(0, 0)
+        ta(2, 1, 1)
+        zb(0, 1)
+        tg(0, 1)
+        ta(1, 1, 1)
+        prod(3, 2)
+        ww("wv", 0, 0)
+        mz(0, 2)
+        mz(0, 0)
+        prod(3, 1)
+        ww("wv", 0, 1)
+        mz(0, 3)
+        ta(2, 1, 0)
+        zb(0, 2)
+        ea(2, 1, 1)
+        tc_(0, 1, 1)
+        ea(1, 1, 1)
+        zb(0, 3)
+        tc_(0, 0, 0)
+        ex(0, 2)
+        qw("wv", 0)
+        tc_(0, 1, 0)
+        ea(2, 1, 0)
+        qa(1, 1)
+        mg(0, 3)
+        ec(0, 1, 1)
         qa(2, 1)
-        ec(1, 1, 0)
-        ta(3, 1, 1)
-        gt(0, 0)
-        ec(1, 1, 1)
-        mz(2, 1)
-        ex(1, 3)
-        mz(2, 2)
-        ea(3, 1, 1)
-        zb(2, 1)
+        mz(1, 3)
+        ec(0, 1, 0)
+        qa(2, 0)
+        tc_(1, 0, 1)
+        ww("wv", 1, 0)
+        prod(3, 3)
+        tc_(1, 1, 1)
+        tc_(1, 0, 0)
+        ex(0, 3)
+        zb(1, 3)
+        ta(3, 1, 0)
+        ec(0, 0, 0)
+        zb(0, 0)
         mz(2, 0)
-        ec(1, 0, 1)
-        zb(2, 2)
-        mz(2, 3)
-        ex(2, 1)
-        tv(0, 0)
-        qa(3, 1)
-        ex(2, 2)
-        mg(2, 2)
-        zb(2, 3)
-        ev(0, 0)
-        mz(3, 0)
+        ex(1, 3)
+        prod(3, 0)
+        mz(2, 1)
+        ex(0, 0)
+        tc_(0, 0, 1)
+        ea(3, 1, 0)
         zb(2, 0)
-        ex(2, 3)
-        mz(3, 1)
-        qc(1, 1)
+        ww("wv", 1, 1)
+        zb(2, 1)
+        ta(3, 0, 1)
+        load_c(2)
+        mz(2, 3)
+        qc(0, 0)
+        ec(0, 0, 1)
+        qw("wv", 1)
+        mz(2, 2)
         ex(2, 0)
+        qc(0, 1)
+        ta(3, 0, 0)
+        ea(3, 0, 1)
+        zb(2, 2)
+        ex(2, 1)
+        ta(3, 1, 1)
+        zb(2, 3)
+        ea(3, 0, 0)
+        mv(0, 0)
+        ex(2, 2)
+        qa(3, 0)
+        mv(0, 1)
+        ea(3, 1, 1)
+        gt(0, 0)
+        tc_(1, 1, 0)
+        ex(2, 3)
+        gt(0, 1)
+        mz(1, 0)
+        tg(0, 3)
+        load_c(3)
+        qa(3, 1)
+        mz(1, 1)
+        ec(1, 0, 1)
+        zb(1, 0)
+        mz(3, 0)
+        ec(1, 1, 1)
+        zb(1, 1)
+        tv(0, 0)
+        ec(1, 0, 0)
+        mz(3, 2)
+        qc(1, 1)
+        ex(1, 0)
         mz(3, 3)
         zb(3, 0)
-        tg(2, 2)
-        tc_(1, 0, 0)
-        zb(3, 1)
-        ex(3, 0)
-        mz(3, 2)
-        zb(3, 3)
-        load_c(3)
-        ec(1, 0, 0)
-        mg(2, 3)
-        ex(3, 1)
+        ex(1, 1)
         zb(3, 2)
-        mv(0, 3)
+        ex(0, 1)
+        mz(3, 1)
+        zb(3, 3)
+        ex(3, 0)
+        mz(1, 2)
+        ec(1, 1, 0)
+        zb(3, 1)
+        mg(0, 2)
         ex(3, 3)
+        zb(1, 2)
+        mg(1, 2)
+        ex(3, 1)
         qc(1, 0)
-        tc_(2, 0, 1)
-        ex(3, 2)
+        mv(0, 3)
+        tg(0, 2)
         max_all()
-        gt(0, 3)
-        tc_(2, 1, 0)
-        ec(2, 0, 1)
         max_diff()
-        mv(1, 0)
+        tg(1, 2)
+        gt(0, 3)
+        mv(0, 2)
         max_corr()
-        tg(2, 3)
+        ex(3, 2)
+        tc_(2, 1, 1)
+        gt(0, 2)
+        ex(1, 2)
+        tc_(2, 1, 0)
+        ev(0, 0)
         tv(0, 1)
         first1()
         first2()
-        ec(2, 1, 0)
-        gt(1, 0)
-        mg(3, 2)
-        ev(0, 1)
-        first3()
-        tc_(2, 1, 1)
-        first4()
-        sc(3, 3)
-        qv(0)
-        mv(1, 2)
-        sc(3, 0)
-        mv(1, 3)
+        tc_(2, 0, 1)
         ec(2, 1, 1)
-        gt(1, 2)
-        mg(3, 3)
-        sc(3, 1)
-        gt(1, 3)
-        tc_(2, 0, 0)
-        sc(3, 2)
-        qc(2, 1)
-        tv(1, 1)
-        sc(2, 2)
-        mg(2, 0)
-        ec(2, 0, 0)
-        sums(3)
-        sc(2, 3)
-        qc(2, 0)
-        tg(2, 0)
-        sc(2, 0)
-        mv(2, 3)
-        pw1(3)
-        sc(2, 1)
-        mv(2, 2)
-        gt(2, 3)
-        sc(1, 1)
-        pw2(3)
-        sums(2)
-        gt(2, 2)
-        sc(1, 2)
-        sc(1, 3)
-        spread(3)
-        sc(1, 0)
-        mg(3, 0)
-        pw1(2)
-        sc(0, 2)
-        bal(3, 0)
-        sums(1)
-        sc(0, 1)
-        pw2(2)
-        bal(3, 2)
-        tg(3, 0)
-        bal(3, 1)
+        first3()
+        first4()
+        mv(1, 2)
+        ev(0, 1)
         sc(0, 3)
-        mv(2, 0)
+        mg(1, 3)
         sc(0, 0)
-        pw1(1)
-        spread(2)
-        ev(1, 1)
-        bal(3, 3)
+        sc(0, 2)
+        qv(0)
+        tc_(2, 0, 0)
+        sc(0, 1)
+        gt(1, 2)
+        sc(3, 3)
+        tg(1, 3)
         mg(1, 1)
-        pw2(1)
-        tg(3, 2)
-        gt(2, 0)
+        sc(1, 2)
+        ec(2, 0, 0)
         sums(0)
-        tg(3, 3)
-        bal(2, 2)
-        tg(1, 1)
-        bal(2, 3)
-        spread(1)
-        bal(2, 0)
-        mv(1, 1)
-        bal(1, 2)
-        tc_(3, 0, 0)
-        bal(1, 0)
+        sc(3, 2)
+        ec(2, 0, 1)
+        sc(1, 0)
+        sc(1, 3)
+        qc(2, 1)
+        mv(1, 3)
+        sc(1, 1)
+        sc(2, 2)
+        pr(0)
         mg(2, 1)
-        ec(3, 0, 0)
-        pw1(0)
-        mg(3, 1)
-        tg(2, 1)
-        bal(1, 1)
-        tc_(3, 1, 1)
+        sc(2, 3)
+        gt(1, 3)
+        sums(1)
+        tg(1, 1)
         pw2(0)
-        tg(3, 1)
-        gt(1, 1)
-        tc_(3, 0, 1)
-        ec(3, 1, 1)
-        bal(1, 3)
-        mv(2, 1)
-        ec(3, 0, 1)
-        bal(2, 1)
+        ec(2, 1, 0)
+        sc(2, 0)
+        mv(1, 1)
+        qc(2, 0)
+        sc(2, 1)
         spread(0)
+        sc(3, 1)
+        gt(1, 1)
+        mg(1, 0)
+        pr(1)
+        bal(0, 2)
+        sums(2)
+        bal(0, 1)
+        tg(1, 0)
+        pw2(1)
+        tg(2, 1)
+        bal(0, 0)
+        mv(1, 0)
+        sc(3, 0)
+        bal(0, 3)
+        spread(1)
+        pr(2)
+        gt(1, 0)
+        sums(3)
+        mass_order()
+        bal(1, 1)
+        pw2(2)
+        bal(1, 0)
         tv(1, 0)
+        mv(2, 1)
+        pr(3)
+        bal(1, 2)
+        spread(2)
+        bal(1, 3)
+        ev(1, 0)
+        pw2(3)
+        tc_(3, 0, 0)
         gt(2, 1)
         tc_(3, 1, 0)
-        bal(0, 0)
-        ev(1, 0)
-        tv(2, 0)
-        bal(0, 3)
+        bal(2, 3)
+        ec(3, 0, 0)
+        mg(2, 0)
         ec(3, 1, 0)
-        tv(2, 1)
-        ev(2, 0)
-        qc(3, 1)
-        ev(2, 1)
+        bal(2, 2)
+        tc_(3, 0, 1)
+        tg(2, 0)
+        bal(2, 1)
+        tc_(3, 1, 1)
+        ec(3, 0, 1)
         qc(3, 0)
-        bal(0, 2)
-        mv(3, 2)
-        qv(2)
-        bal(0, 1)
-        mv(3, 3)
-        gt(3, 2)
-        mv(3, 0)
-        gt(3, 3)
-        mv(3, 1)
+        spread(3)
+        mv(2, 0)
+        ec(3, 1, 1)
+        bal(2, 0)
+        mg(2, 3)
+        bal(3, 1)
+        mg(3, 3)
+        gt(2, 0)
+        tg(2, 3)
+        tv(1, 1)
+        bal(3, 2)
+        tg(3, 3)
+        tv(2, 0)
+        mv(2, 3)
+        bal(3, 0)
+        ev(1, 1)
+        mg(3, 0)
+        bal(3, 3)
+        ev(2, 0)
+        mg(3, 1)
+        gt(2, 3)
+        tg(3, 0)
         second1()
         qv(1)
-        tv(3, 1)
+        mg(2, 2)
+        tg(3, 1)
         second2()
-        gt(3, 1)
-        ev(3, 1)
-        weigh(3, 0)
-        weigh(3, 1)
-        tp(3, 0)
+        qc(3, 1)
+        mg(3, 2)
+        tg(2, 2)
         weigh(0, 1)
-        ep(3, 0)
-        tp(3, 1)
-        gt(3, 0)
-        ep(3, 1)
+        mv(3, 3)
+        tg(3, 2)
+        mv(3, 0)
+        weigh(3, 0)
         tp(0, 1)
-        weigh(1, 0)
-        tv(3, 0)
+        mv(3, 1)
         ep(0, 1)
-        qp(3)
+        gt(3, 0)
+        tp(3, 0)
+        gt(3, 3)
+        mv(2, 2)
+        ep(3, 0)
+        gt(3, 1)
+        mv(3, 2)
+        weigh(3, 1)
+        tv(3, 0)
+        qp(3, 0)
         ev(3, 0)
-        tp(1, 0)
-        weigh(0, 0)
-        ep(1, 0)
-        qv(3)
-        tp(0, 0)
-        weigh(1, 1)
-        my(3)
-        ep(0, 0)
+        tp(3, 1)
+        gt(2, 2)
+        my(3, 0)
+        gt(3, 2)
+        ep(3, 1)
+        tv(2, 1)
         weigh(2, 1)
-        weigh(2, 0)
-        tp(1, 1)
+        tv(3, 1)
+        ev(2, 1)
+        qp(3, 1)
+        ev(3, 1)
         tp(2, 1)
-        qp(0)
-        ep(1, 1)
-        tp(2, 0)
-        fin(3)
+        weigh(2, 0)
         ep(2, 1)
-        my(0)
-        qp(1)
+        qv(2)
+        tp(2, 0)
+        qv(3)
+        weigh(0, 0)
         ep(2, 0)
+        my(3, 1)
         qp(2)
-        my(1)
-        fin(0)
+        tp(0, 0)
+        weigh(1, 0)
         my(2)
-        fin(1)
+        ep(0, 0)
+        weigh(1, 1)
+        tp(1, 0)
+        qp(0)
+        ep(1, 0)
+        tp(1, 1)
+        fin(3)
+        my(0)
+        ep(1, 1)
         fin(2)
+        qp(1)
+        fin(0)
+        my(1)
+        fin(1)

@@ -115,7 +115,7 @@ def tile_sinkhorn_slot_mixing_f5_kernel(
 
         def load_scale(g):
             cols = slice(512 * g, 512 * (g + 1))
-            nc.sync.dma_start(out=scale[:, cols], in_=a_scale[:, cols].rearrange("o k -> (o k)").partition_broadcast(P))
+            nc.scalar.dma_start(out=scale[:, cols], in_=a_scale[:, cols].rearrange("o k -> (o k)").partition_broadcast(P))
 
         def load_c(i):
             c_raw[i] = work.tile([P, 4, C], BF16, name="c_raw", tag="c_raw", bufs=2)
@@ -166,8 +166,8 @@ def tile_sinkhorn_slot_mixing_f5_kernel(
 
         def ww(key, g, h):
             nc.scalar.copy(
-                out=group((key, g))[:, 1024 * h : 1024 * (h + 1)].rearrange("p (f j) -> p f j", j=4),
-                in_=w_raw[key][:, g, :, 256 * h : 256 * (h + 1)].rearrange("p j f -> p f j"),
+                out=group((key, g))[:, 1024 * h : 1024 * (h + 1)].rearrange("p (c i j) -> p c j i", i=4, j=4),
+                in_=w_raw[key][:, g, :, 256 * h : 256 * (h + 1)].rearrange("p j (c i) -> p c j i", i=4),
             )
 
         def quant(dst, plane, key):
@@ -367,373 +367,375 @@ def tile_sinkhorn_slot_mixing_f5_kernel(
         ctx.enter_context(tc.manual_schedule())
 
         nc.sync.dma_start(out=ab[0][:, 0:2, :], in_=a_view[0][:, 0:2, :])
+        load_scale(0)
+        nc.sync.dma_start(out=ab[0][:, 2:4, :], in_=a_view[0][:, 2:4, :])
+        load_scale(1)
         nc.scalar.dma_start(out=vec[0:4, :], in_=bg.rearrange("(r f) -> r f", f=P))
         nc.scalar.dma_start(out=vec[4:8, :], in_=beta.rearrange("(r f) -> r f", f=P))
         nc.scalar.activation(out=dummy[:], in_=dummy[:], func=ACT.Exp)
-        load_scale(0)
-        load_scale(1)
-        nc.sync.dma_start(out=ab[0][:, 2:4, :], in_=a_view[0][:, 2:4, :])
         nc.sync.dma_start(out=ab[1][:], in_=a_view[1])
         nc.sync.dma_start(out=e_raw[:], in_=e.rearrange("(s p) d -> p s d", p=P))
         load_w("wg", wg)
         nc.sync.dma_start(out=ab[2][:], in_=a_view[2])
         nc.sync.dma_start(out=ab[3][:], in_=a_view[3])
 
-        prod(0, 0, 0)
-        prod(0, 0, 1)
-        prod(0, 1, 1)
         prod(0, 1, 0)
-        ta(0, 0, 1)
-        prod(1, 2)
-        ta(0, 0, 0)
-        ea(0, 0, 1)
-        prod(0, 2)
-        ea(0, 0, 0)
-        te(0, 1)
-        prod(0, 3)
-        te(1, 1)
-        ee(0, 1)
-        prod(1, 1)
-        te(1, 0)
-        ee(1, 1)
-        ta(0, 1, 1)
-        ee(1, 0)
-        prod(1, 0)
-        ta(0, 1, 0)
-        ea(0, 1, 1)
-        te(0, 0)
-        qe(1)
-        ea(0, 1, 0)
-        ta(1, 0, 1)
-        prod(2, 0)
-        ee(0, 0)
-        ta(1, 0, 0)
-        ww("wg", 1, 0)
+        prod(0, 2, 0)
+        prod(0, 3, 0)
         vec_t()
-        qa(0, 1)
-        vec_beta()
-        prod(2, 1)
-        ww("wg", 1, 1)
-        prod(1, 3)
-        ww("wg", 0, 0)
-        ta(2, 0, 1)
-        ta(2, 0, 0)
-        qw("wg", 1)
-        ww("wg", 0, 1)
+        prod(0, 0, 0)
+        ta(0, 1, 0)
+        prod(0, 1, 1)
+        ta(0, 0, 0)
+        prod(0, 0, 1)
+        ea(0, 1, 0)
+        prod(0, 3, 1)
+        ea(0, 0, 0)
+        ta(0, 0, 1)
+        prod(0, 2, 1)
+        prod(1, 1)
+        ea(0, 0, 1)
+        ta(0, 1, 1)
+        te(0, 0)
         qa(0, 0)
-        ea(2, 0, 1)
-        vec_bg()
+        ea(0, 1, 1)
+        te(0, 1)
+        prod(1, 0)
+        ee(0, 0)
+        te(1, 0)
+        ee(0, 1)
+        te(1, 1)
+        qa(0, 1)
+        ww("wg", 0, 0)
+        ta(1, 0, 0)
         qe(0)
-        load_w("wv", wv)
+        ta(1, 0, 1)
+        prod(1, 3)
+        ee(1, 0)
+        ea(1, 0, 0)
+        prod(2, 1)
+        ea(1, 0, 1)
+        ee(1, 1)
+        prod(1, 2)
+        ww("wg", 0, 1)
+        qe(1)
         ta(1, 1, 0)
+        prod(2, 0)
+        ww("wg", 1, 0)
+        mz(0, 0)
+        prod(2, 3)
+        ea(1, 1, 0)
+        ta(2, 0, 0)
+        ww("wg", 1, 1)
+        ta(1, 1, 1)
+        vec_beta()
+        qa(1, 0)
+        mz(0, 1)
+        zb(0, 0)
+        ea(2, 0, 0)
+        load_w("wv", wv)
+        mz(0, 2)
         load_c(0)
         load_c(1)
         nc.sync.dma_start(out=mass_n[:], in_=mass.partition_broadcast(P))
+        qw("wg", 1)
         nc.sync.dma_start(out=bo_b[:], in_=bo.partition_broadcast(P))
-        ea(1, 0, 1)
-        qw("wg", 0)
-        mz(0, 1)
-        ea(1, 0, 0)
-        prod(2, 3)
-        ea(1, 1, 0)
-        mg(0, 0)
-        ea(2, 0, 0)
-        prod(2, 2)
-        mg(0, 1)
-        qa(1, 0)
-        tg(0, 0)
-        ta(2, 1, 1)
-        zb(0, 1)
-        tg(0, 1)
-        ta(1, 1, 1)
-        prod(3, 2)
-        ww("wv", 0, 0)
-        mz(0, 2)
-        mz(0, 0)
-        prod(3, 1)
-        ww("wv", 0, 1)
-        mz(0, 3)
-        ta(2, 1, 0)
-        zb(0, 2)
-        ea(2, 1, 1)
-        tc_(0, 1, 1)
         ea(1, 1, 1)
-        zb(0, 3)
-        tc_(0, 0, 0)
-        ex(0, 2)
-        qw("wv", 0)
-        tc_(0, 1, 0)
-        ea(2, 1, 0)
-        qa(1, 1)
-        mg(0, 3)
-        ec(0, 1, 1)
-        qa(2, 1)
-        mz(1, 3)
-        ec(0, 1, 0)
-        qa(2, 0)
-        tc_(1, 0, 1)
-        ww("wv", 1, 0)
-        prod(3, 3)
-        tc_(1, 1, 1)
-        tc_(1, 0, 0)
-        ex(0, 3)
-        zb(1, 3)
-        ta(3, 1, 0)
-        ec(0, 0, 0)
-        zb(0, 0)
-        mz(2, 0)
-        ex(1, 3)
-        prod(3, 0)
-        mz(2, 1)
+        mz(0, 3)
+        zb(0, 1)
         ex(0, 0)
-        tc_(0, 0, 1)
-        ea(3, 1, 0)
-        zb(2, 0)
+        ta(2, 0, 1)
+        qa(1, 1)
+        ex(0, 1)
+        zb(0, 3)
+        mz(1, 0)
+        ea(2, 0, 1)
+        zb(0, 2)
+        ex(0, 3)
+        mz(1, 2)
+        prod(2, 2)
+        ex(0, 2)
+        mz(1, 3)
+        ww("wv", 1, 0)
+        zb(1, 2)
+        ta(2, 1, 0)
+        prod(3, 2)
+        mz(1, 1)
+        ex(1, 2)
+        ta(2, 1, 1)
+        ea(2, 1, 0)
+        qw("wg", 0)
         ww("wv", 1, 1)
+        tc_(0, 1, 1)
+        zb(1, 1)
+        tc_(0, 0, 0)
+        qa(2, 0)
+        mg(0, 2)
+        ex(1, 1)
+        qw("wv", 1)
+        ea(2, 1, 1)
+        tc_(0, 0, 1)
+        zb(1, 0)
+        ww("wv", 0, 1)
+        tc_(1, 1, 0)
+        qa(2, 1)
+        mg(0, 3)
+        vec_bg()
+        prod(3, 3)
+        ec(0, 0, 1)
+        tc_(1, 1, 1)
+        tg(0, 2)
+        prod(3, 0)
+        tc_(0, 1, 0)
+        tg(0, 3)
+        mz(2, 2)
+        ex(1, 0)
+        load_c(2)
+        prod(3, 1)
+        mg(0, 0)
+        ec(0, 1, 0)
+        ec(0, 0, 0)
+        ta(3, 1, 0)
+        zb(2, 2)
+        tg(0, 0)
+        ta(3, 1, 1)
+        qc(0, 0)
+        ec(0, 1, 1)
+        mg(1, 3)
+        zb(1, 3)
+        ea(3, 1, 0)
+        mz(2, 1)
+        qc(0, 1)
+        ea(3, 1, 1)
+        mz(2, 3)
+        ex(1, 3)
         zb(2, 1)
         ta(3, 0, 1)
-        load_c(2)
-        mz(2, 3)
-        qc(0, 0)
-        ec(0, 0, 1)
-        qw("wv", 1)
-        mz(2, 2)
-        ex(2, 0)
-        qc(0, 1)
-        ta(3, 0, 0)
-        ea(3, 0, 1)
-        zb(2, 2)
-        ex(2, 1)
-        ta(3, 1, 1)
-        zb(2, 3)
-        ea(3, 0, 0)
-        mv(0, 0)
-        ex(2, 2)
-        qa(3, 0)
-        mv(0, 1)
-        ea(3, 1, 1)
-        gt(0, 0)
-        tc_(1, 1, 0)
-        ex(2, 3)
-        gt(0, 1)
-        mz(1, 0)
-        tg(0, 3)
-        load_c(3)
-        qa(3, 1)
-        mz(1, 1)
-        ec(1, 0, 1)
-        zb(1, 0)
-        mz(3, 0)
-        ec(1, 1, 1)
-        zb(1, 1)
-        tv(0, 0)
-        ec(1, 0, 0)
-        mz(3, 2)
-        qc(1, 1)
-        ex(1, 0)
-        mz(3, 3)
-        zb(3, 0)
-        ex(1, 1)
-        zb(3, 2)
-        ex(0, 1)
-        mz(3, 1)
-        zb(3, 3)
-        ex(3, 0)
-        mz(1, 2)
-        ec(1, 1, 0)
-        zb(3, 1)
-        mg(0, 2)
-        ex(3, 3)
-        zb(1, 2)
-        mg(1, 2)
-        ex(3, 1)
-        qc(1, 0)
-        mv(0, 3)
-        tg(0, 2)
-        max_all()
-        max_diff()
-        tg(1, 2)
-        gt(0, 3)
-        mv(0, 2)
-        max_corr()
-        ex(3, 2)
-        tc_(2, 1, 1)
-        gt(0, 2)
-        ex(1, 2)
-        tc_(2, 1, 0)
-        ev(0, 0)
-        tv(0, 1)
-        first1()
-        first2()
-        tc_(2, 0, 1)
-        ec(2, 1, 1)
-        first3()
-        first4()
-        mv(1, 2)
-        ev(0, 1)
-        sc(0, 3)
-        mg(1, 3)
-        sc(0, 0)
-        sc(0, 2)
-        qv(0)
-        tc_(2, 0, 0)
-        sc(0, 1)
-        gt(1, 2)
-        sc(3, 3)
         tg(1, 3)
+        zb(2, 3)
+        ta(3, 0, 0)
+        ex(2, 1)
+        mg(0, 1)
+        ea(3, 0, 1)
         mg(1, 1)
-        sc(1, 2)
+        ea(3, 0, 0)
+        qa(3, 1)
+        mz(2, 0)
+        tg(0, 1)
+        qa(3, 0)
+        tc_(1, 0, 1)
+        ex(2, 3)
+        zb(2, 0)
+        mz(3, 3)
+        ex(2, 2)
+        mz(3, 2)
+        ex(2, 0)
+        zb(3, 3)
+        tc_(1, 0, 0)
+        ww("wv", 0, 0)
+        zb(3, 2)
+        mz(3, 1)
+        load_c(3)
+        ex(3, 3)
+        mz(3, 0)
+        qw("wv", 0)
+        ex(3, 2)
+        zb(3, 1)
+        ec(1, 0, 0)
+        zb(3, 0)
+        mv(0, 3)
+        ex(3, 1)
+        max_all()
+        mv(0, 2)
+        ex(3, 0)
+        max_diff()
+        gt(0, 3)
+        max_corr()
+        ec(1, 1, 1)
+        first1()
+        gt(0, 2)
+        mv(0, 1)
+        ec(1, 1, 0)
+        first2()
+        mv(0, 0)
+        first3()
+        ec(1, 0, 1)
+        first4()
+        gt(0, 1)
+        sc(0, 2)
+        tc_(2, 0, 0)
+        sc(0, 0)
+        qc(1, 0)
+        sc(0, 3)
+        tc_(2, 1, 1)
+        sc(0, 1)
+        gt(0, 0)
+        tc_(2, 0, 1)
         ec(2, 0, 0)
+        sc(1, 3)
+        qc(1, 1)
         sums(0)
+        ec(2, 1, 1)
+        sc(1, 2)
+        sc(1, 1)
         sc(3, 2)
         ec(2, 0, 1)
-        sc(1, 0)
-        sc(1, 3)
-        qc(2, 1)
         mv(1, 3)
-        sc(1, 1)
         sc(2, 2)
         pr(0)
-        mg(2, 1)
-        sc(2, 3)
+        mg(2, 3)
+        qc(2, 1)
+        sc(3, 3)
+        tc_(2, 1, 0)
+        sc(1, 0)
         gt(1, 3)
-        sums(1)
-        tg(1, 1)
         pw2(0)
-        ec(2, 1, 0)
         sc(2, 0)
-        mv(1, 1)
-        qc(2, 0)
+        tv(0, 1)
+        sums(1)
+        ec(2, 1, 0)
+        sc(2, 3)
         sc(2, 1)
+        qc(2, 0)
+        tg(1, 1)
         spread(0)
-        sc(3, 1)
-        gt(1, 1)
         mg(1, 0)
         pr(1)
         bal(0, 2)
-        sums(2)
-        bal(0, 1)
-        tg(1, 0)
-        pw2(1)
-        tg(2, 1)
-        bal(0, 0)
-        mv(1, 0)
+        mv(1, 1)
         sc(3, 0)
+        bal(0, 1)
+        sums(2)
+        pw2(1)
+        tg(1, 0)
         bal(0, 3)
+        ev(0, 1)
+        bal(0, 0)
         spread(1)
+        sc(3, 1)
+        gt(1, 1)
+        mv(1, 0)
         pr(2)
-        gt(1, 0)
+        bal(1, 1)
         sums(3)
         mass_order()
-        bal(1, 1)
+        gt(1, 0)
         pw2(2)
-        bal(1, 0)
-        tv(1, 0)
-        mv(2, 1)
-        pr(3)
         bal(1, 2)
-        spread(2)
-        bal(1, 3)
-        ev(1, 0)
-        pw2(3)
-        tc_(3, 0, 0)
-        gt(2, 1)
-        tc_(3, 1, 0)
-        bal(2, 3)
-        ec(3, 0, 0)
-        mg(2, 0)
-        ec(3, 1, 0)
-        bal(2, 2)
-        tc_(3, 0, 1)
-        tg(2, 0)
-        bal(2, 1)
-        tc_(3, 1, 1)
-        ec(3, 0, 1)
-        qc(3, 0)
-        spread(3)
-        mv(2, 0)
-        ec(3, 1, 1)
-        bal(2, 0)
-        mg(2, 3)
-        bal(3, 1)
-        mg(3, 3)
-        gt(2, 0)
+        mg(1, 2)
         tg(2, 3)
-        tv(1, 1)
-        bal(3, 2)
+        bal(1, 3)
+        pr(3)
+        spread(2)
+        bal(1, 0)
+        mg(2, 1)
+        tg(1, 2)
+        bal(2, 1)
+        pw2(3)
+        mg(3, 3)
+        tg(2, 1)
+        bal(2, 3)
+        mv(1, 2)
         tg(3, 3)
-        tv(2, 0)
-        mv(2, 3)
-        bal(3, 0)
-        ev(1, 1)
-        mg(3, 0)
+        bal(2, 2)
+        spread(3)
+        tc_(3, 0, 1)
+        bal(2, 0)
+        tc_(3, 1, 0)
         bal(3, 3)
-        ev(2, 0)
-        mg(3, 1)
-        gt(2, 3)
-        tg(3, 0)
-        second1()
-        qv(1)
+        ec(3, 0, 1)
+        tc_(3, 1, 1)
+        bal(3, 1)
+        ec(3, 1, 0)
+        tc_(3, 0, 0)
+        ec(3, 1, 1)
+        bal(3, 2)
+        mv(2, 3)
+        ec(3, 0, 0)
+        bal(3, 0)
+        gt(1, 2)
         mg(2, 2)
-        tg(3, 1)
-        second2()
+        second1()
         qc(3, 1)
         mg(3, 2)
+        second2()
+        qc(3, 0)
         tg(2, 2)
+        tv(1, 0)
         weigh(0, 1)
-        mv(3, 3)
         tg(3, 2)
-        mv(3, 0)
-        weigh(3, 0)
-        tp(0, 1)
-        mv(3, 1)
-        ep(0, 1)
-        gt(3, 0)
-        tp(3, 0)
-        gt(3, 3)
-        mv(2, 2)
-        ep(3, 0)
-        gt(3, 1)
-        mv(3, 2)
+        tv(0, 0)
+        mv(3, 3)
+        ev(1, 0)
         weigh(3, 1)
-        tv(3, 0)
-        qp(3, 0)
-        ev(3, 0)
+        mv(2, 2)
+        ev(0, 0)
+        tp(0, 1)
+        weigh(3, 0)
+        tv(1, 1)
         tp(3, 1)
-        gt(2, 2)
-        my(3, 0)
-        gt(3, 2)
+        ep(0, 1)
+        ev(1, 1)
+        gt(2, 3)
+        tp(3, 0)
         ep(3, 1)
-        tv(2, 1)
-        weigh(2, 1)
-        tv(3, 1)
-        ev(2, 1)
-        qp(3, 1)
-        ev(3, 1)
-        tp(2, 1)
-        weigh(2, 0)
-        ep(2, 1)
-        qv(2)
-        tp(2, 0)
-        qv(3)
-        weigh(0, 0)
-        ep(2, 0)
-        my(3, 1)
-        qp(2)
-        tp(0, 0)
+        gt(2, 2)
+        mg(3, 1)
+        ep(3, 0)
         weigh(1, 0)
-        my(2)
-        ep(0, 0)
+        tv(2, 1)
+        tg(3, 1)
+        mv(2, 1)
         weigh(1, 1)
         tp(1, 0)
-        qp(0)
-        ep(1, 0)
+        mv(3, 1)
+        qp(3, 0)
+        gt(3, 3)
         tp(1, 1)
-        fin(3)
-        my(0)
+        qp(3, 1)
+        mg(2, 0)
+        gt(2, 1)
+        ep(1, 0)
+        qv(0)
+        mg(3, 0)
         ep(1, 1)
-        fin(2)
+        gt(3, 1)
+        tg(2, 0)
+        weigh(2, 1)
+        tg(3, 0)
+        mv(3, 2)
+        mv(2, 0)
+        ev(2, 1)
+        weigh(2, 0)
+        mv(3, 0)
+        tp(2, 1)
+        gt(2, 0)
+        tp(2, 0)
+        gt(3, 0)
+        tv(2, 0)
+        gt(3, 2)
+        tv(3, 0)
+        ev(2, 0)
+        qv(1)
+        tv(3, 1)
+        weigh(0, 0)
+        ev(3, 0)
+        my(3, 0)
+        ev(3, 1)
+        qv(2)
+        tp(0, 0)
+        qv(3)
+        ep(2, 0)
         qp(1)
-        fin(0)
+        ep(2, 1)
+        my(3, 1)
+        ep(0, 0)
         my(1)
+        qp(2)
+        qp(0)
+        my(2)
+        fin(3)
         fin(1)
+        my(0)
+        fin(2)
+        fin(0)

@@ -46,7 +46,6 @@ def tile_sinkhorn_slot_mixing_f5_kernel(
 
         scale = keep.tile([P, D], F32, name="scale")
         ab = [keep.tile([P, 4, D], U8, name="ab%d" % i) for i in range(CH)]
-        e_raw = keep.tile([P, ST, D], BF16, name="e_raw")
         vec = keep.tile([P, P], BF16, name="vec")
         mass_n = keep.tile([P, T], BF16, name="mass_n")
         mass_p = keep.tile([P, T], BF16, name="mass_p")
@@ -88,6 +87,8 @@ def tile_sinkhorn_slot_mixing_f5_kernel(
         codes = {}
         pt = {}
         pcodes = {}
+        cr = {}
+        raw = {}
         small = {}
         w_codes = {"wg": (wg_codes, wg_planes), "wv": (wv_codes, wv_planes)}
 
@@ -117,12 +118,16 @@ def tile_sinkhorn_slot_mixing_f5_kernel(
             cols = slice(512 * g, 512 * (g + 1))
             nc.scalar.dma_start(out=scale[:, cols], in_=a_scale[:, cols].rearrange("o k -> (o k)").partition_broadcast(P))
 
+        def load_e():
+            raw["e"] = work.tile([P, ST, D], BF16, name="e_raw", tag="raw", bufs=4)
+            nc.sync.dma_start(out=raw["e"][:], in_=e.rearrange("(s p) d -> p s d", p=P))
+
         def load_c(i):
-            c_raw[i] = work.tile([P, 4, C], BF16, name="c_raw", tag="c_raw", bufs=2)
+            c_raw[i] = work.tile([P, 4, C], BF16, name="c_raw", tag="raw", bufs=4)
             nc.sync.dma_start(out=c_raw[i][:], in_=c_view[i])
 
         def load_w(key, w):
-            w_raw[key] = work.tile([P, KP, 4, F], BF16, name="w_raw", tag="w_raw", bufs=1)
+            w_raw[key] = work.tile([P, KP, 4, F], BF16, name="w_raw", tag="raw", bufs=4)
             nc.sync.dma_start(out=w_raw[key][:], in_=w.rearrange("(g p j) f -> p g j f", p=P, j=4))
 
         def prod(i, t, g=None):
@@ -147,7 +152,7 @@ def tile_sinkhorn_slot_mixing_f5_kernel(
             weave("c", (i, h, g), ("c", i, g), h, 1)
 
         def te(g, h):
-            turn("e", (g, h), lambda a, u: step2(e_raw[:, 2 * h + a, :].bitcast(F32), g, u))
+            turn("e", (g, h), lambda a, u: step2(raw["e"][:, 2 * h + a, :].bitcast(F32), g, u))
 
         def ee(g, h):
             weave("e", (g, h), ("e", g), h, 0)
@@ -350,6 +355,15 @@ def tile_sinkhorn_slot_mixing_f5_kernel(
                 op0=ALU.mult, op1=ALU.mult,
             )
 
+        def gm(s, i):
+            nc.gpsimd.tensor_tensor(out=ew[:, s, chunk(i)], in0=ew[:, s, chunk(i)], in1=mass_p[:, chunk(i)], op=ALU.mult)
+
+        def ws(s, h):
+            if s not in pt:
+                pt[s] = work.tile([P, T], BF16, name="pt", tag="pt", bufs=2)
+            half = slice(T // 2 * h, T // 2 * (h + 1))
+            nc.scalar.activation(out=pt[s][:, half], in_=ew[:, s, half], func=ACT.Copy, scale=small["second"][:, s : s + 1])
+
         def my(s, h=None):
             if ("y", s) not in banks:
                 bank(("y", s), "mm")
@@ -374,368 +388,376 @@ def tile_sinkhorn_slot_mixing_f5_kernel(
         nc.scalar.dma_start(out=vec[4:8, :], in_=beta.rearrange("(r f) -> r f", f=P))
         nc.scalar.activation(out=dummy[:], in_=dummy[:], func=ACT.Exp)
         nc.sync.dma_start(out=ab[1][:], in_=a_view[1])
-        nc.sync.dma_start(out=e_raw[:], in_=e.rearrange("(s p) d -> p s d", p=P))
+        load_e()
         load_w("wg", wg)
         nc.sync.dma_start(out=ab[2][:], in_=a_view[2])
         nc.sync.dma_start(out=ab[3][:], in_=a_view[3])
 
-        prod(0, 1, 0)
-        prod(0, 2, 0)
-        prod(0, 3, 0)
-        vec_t()
+        load_w("wv", wv)
+        load_c(0)
         prod(0, 0, 0)
-        ta(0, 1, 0)
-        prod(0, 1, 1)
+        prod(0, 3, 0)
+        prod(0, 1, 0)
+        vec_t()
+        prod(0, 2, 0)
         ta(0, 0, 0)
-        prod(0, 0, 1)
-        ea(0, 1, 0)
         prod(0, 3, 1)
+        ta(0, 1, 0)
+        prod(0, 0, 1)
         ea(0, 0, 0)
-        ta(0, 0, 1)
         prod(0, 2, 1)
-        prod(1, 1)
-        ea(0, 0, 1)
+        ea(0, 1, 0)
+        prod(0, 1, 1)
         ta(0, 1, 1)
-        te(0, 0)
-        qa(0, 0)
+        vec_beta()
+        prod(1, 3)
+        ta(0, 0, 1)
         ea(0, 1, 1)
         te(0, 1)
-        prod(1, 0)
-        ee(0, 0)
+        prod(1, 1)
+        ea(0, 0, 1)
         te(1, 0)
         ee(0, 1)
         te(1, 1)
         qa(0, 1)
-        ww("wg", 0, 0)
-        ta(1, 0, 0)
-        qe(0)
-        ta(1, 0, 1)
-        prod(1, 3)
         ee(1, 0)
-        ea(1, 0, 0)
-        prod(2, 1)
-        ea(1, 0, 1)
-        ee(1, 1)
-        prod(1, 2)
+        te(0, 0)
+        prod(1, 0)
         ww("wg", 0, 1)
-        qe(1)
-        ta(1, 1, 0)
-        prod(2, 0)
-        ww("wg", 1, 0)
-        mz(0, 0)
-        prod(2, 3)
-        ea(1, 1, 0)
-        ta(2, 0, 0)
-        ww("wg", 1, 1)
-        ta(1, 1, 1)
-        vec_beta()
-        qa(1, 0)
-        mz(0, 1)
-        zb(0, 0)
-        ea(2, 0, 0)
-        load_w("wv", wv)
-        mz(0, 2)
-        load_c(0)
         load_c(1)
         nc.sync.dma_start(out=mass_n[:], in_=mass.partition_broadcast(P))
-        qw("wg", 1)
         nc.sync.dma_start(out=bo_b[:], in_=bo.partition_broadcast(P))
+        prod(1, 2)
+        ee(0, 0)
+        ta(1, 0, 1)
+        ee(1, 1)
+        ta(1, 0, 0)
+        qe(0)
+        ww("wg", 0, 0)
+        ta(1, 1, 1)
+        qe(1)
+        ta(1, 1, 0)
+        qa(0, 0)
+        ea(1, 0, 1)
+        qw("wg", 0)
+        ea(1, 1, 0)
+        mz(0, 0)
+        prod(2, 1)
+        ww("wv", 0, 1)
+        mz(0, 1)
+        prod(2, 3)
+        ww("wv", 1, 1)
+        mz(0, 2)
+        zb(0, 0)
+        ww("wv", 0, 0)
+        tc_(0, 1, 0)
+        prod(2, 2)
+        tc_(0, 1, 1)
         ea(1, 1, 1)
         mz(0, 3)
-        zb(0, 1)
-        ex(0, 0)
-        ta(2, 0, 1)
-        qa(1, 1)
-        ex(0, 1)
-        zb(0, 3)
-        mz(1, 0)
-        ea(2, 0, 1)
         zb(0, 2)
-        ex(0, 3)
-        mz(1, 2)
-        prod(2, 2)
-        ex(0, 2)
-        mz(1, 3)
-        ww("wv", 1, 0)
-        zb(1, 2)
+        ea(1, 0, 0)
         ta(2, 1, 0)
-        prod(3, 2)
-        mz(1, 1)
-        ex(1, 2)
-        ta(2, 1, 1)
-        ea(2, 1, 0)
-        qw("wg", 0)
-        ww("wv", 1, 1)
-        tc_(0, 1, 1)
-        zb(1, 1)
-        tc_(0, 0, 0)
-        qa(2, 0)
-        mg(0, 2)
-        ex(1, 1)
-        qw("wv", 1)
-        ea(2, 1, 1)
-        tc_(0, 0, 1)
-        zb(1, 0)
-        ww("wv", 0, 1)
-        tc_(1, 1, 0)
-        qa(2, 1)
-        mg(0, 3)
-        vec_bg()
-        prod(3, 3)
-        ec(0, 0, 1)
+        qa(1, 1)
+        ex(0, 0)
         tc_(1, 1, 1)
-        tg(0, 2)
-        prod(3, 0)
-        tc_(0, 1, 0)
-        tg(0, 3)
-        mz(2, 2)
-        ex(1, 0)
-        load_c(2)
-        prod(3, 1)
-        mg(0, 0)
-        ec(0, 1, 0)
-        ec(0, 0, 0)
-        ta(3, 1, 0)
-        zb(2, 2)
-        tg(0, 0)
-        ta(3, 1, 1)
-        qc(0, 0)
-        ec(0, 1, 1)
-        mg(1, 3)
-        zb(1, 3)
-        ea(3, 1, 0)
-        mz(2, 1)
-        qc(0, 1)
-        ea(3, 1, 1)
-        mz(2, 3)
-        ex(1, 3)
-        zb(2, 1)
-        ta(3, 0, 1)
-        tg(1, 3)
-        zb(2, 3)
-        ta(3, 0, 0)
-        ex(2, 1)
-        mg(0, 1)
-        ea(3, 0, 1)
-        mg(1, 1)
-        ea(3, 0, 0)
-        qa(3, 1)
-        mz(2, 0)
-        tg(0, 1)
-        qa(3, 0)
-        tc_(1, 0, 1)
-        ex(2, 3)
-        zb(2, 0)
-        mz(3, 3)
-        ex(2, 2)
-        mz(3, 2)
-        ex(2, 0)
-        zb(3, 3)
-        tc_(1, 0, 0)
-        ww("wv", 0, 0)
-        zb(3, 2)
-        mz(3, 1)
-        load_c(3)
-        ex(3, 3)
-        mz(3, 0)
+        zb(0, 3)
+        ex(0, 2)
         qw("wv", 0)
-        ex(3, 2)
-        zb(3, 1)
+        ww("wv", 1, 0)
+        qa(1, 0)
+        ec(0, 1, 0)
+        vec_bg()
+        prod(3, 0)
+        mz(1, 0)
+        load_c(2)
+        ec(0, 1, 1)
+        ex(0, 3)
+        qw("wv", 1)
+        tc_(1, 0, 0)
+        ea(2, 1, 0)
+        prod(2, 0)
+        mz(1, 1)
+        ww("wg", 1, 1)
+        ta(2, 1, 1)
+        zb(1, 0)
+        ta(2, 0, 0)
+        ww("wg", 1, 0)
+        zb(0, 1)
+        ta(2, 0, 1)
+        prod(3, 1)
+        mz(1, 3)
+        ex(0, 1)
+        load_c(3)
+        ea(2, 0, 0)
+        mz(1, 2)
+        qw("wg", 1)
+        ex(1, 0)
+        zb(1, 3)
+        tc_(0, 0, 1)
+        ea(2, 0, 1)
+        qa(2, 0)
+        mg(0, 3)
+        ea(2, 1, 1)
+        zb(1, 2)
+        ta(3, 0, 1)
         ec(1, 0, 0)
-        zb(3, 0)
-        mv(0, 3)
-        ex(3, 1)
-        max_all()
-        mv(0, 2)
-        ex(3, 0)
-        max_diff()
-        gt(0, 3)
-        max_corr()
+        qa(2, 1)
+        mg(0, 2)
+        tg(0, 3)
+        prod(3, 2)
+        ea(3, 0, 1)
+        tc_(0, 0, 0)
+        tg(0, 2)
+        mz(2, 2)
+        prod(3, 3)
+        ex(1, 2)
+        mz(2, 3)
+        ec(0, 0, 0)
+        zb(2, 2)
+        ta(3, 0, 0)
+        ec(0, 0, 1)
+        qc(0, 0)
+        ta(3, 1, 0)
+        ex(2, 2)
+        zb(2, 3)
+        ta(3, 1, 1)
+        ea(3, 0, 0)
+        mz(2, 0)
+        qc(0, 1)
+        ea(3, 1, 0)
+        zb(1, 1)
+        mg(0, 0)
+        ea(3, 1, 1)
+        tc_(1, 0, 1)
+        qa(3, 0)
         ec(1, 1, 1)
-        first1()
-        gt(0, 2)
-        mv(0, 1)
-        ec(1, 1, 0)
-        first2()
-        mv(0, 0)
-        first3()
+        qa(3, 1)
+        mz(2, 1)
+        ex(1, 1)
+        zb(2, 0)
+        tc_(1, 1, 0)
+        tg(0, 0)
+        zb(2, 1)
         ec(1, 0, 1)
-        first4()
-        gt(0, 1)
-        sc(0, 2)
-        tc_(2, 0, 0)
-        sc(0, 0)
-        qc(1, 0)
-        sc(0, 3)
-        tc_(2, 1, 1)
-        sc(0, 1)
-        gt(0, 0)
-        tc_(2, 0, 1)
-        ec(2, 0, 0)
-        sc(1, 3)
+        mz(3, 1)
+        ex(2, 0)
+        mv(0, 2)
         qc(1, 1)
-        sums(0)
-        ec(2, 1, 1)
-        sc(1, 2)
-        sc(1, 1)
-        sc(3, 2)
-        ec(2, 0, 1)
-        mv(1, 3)
-        sc(2, 2)
-        pr(0)
-        mg(2, 3)
-        qc(2, 1)
-        sc(3, 3)
-        tc_(2, 1, 0)
-        sc(1, 0)
-        gt(1, 3)
-        pw2(0)
-        sc(2, 0)
+        ec(1, 1, 0)
+        mz(3, 0)
+        zb(3, 1)
+        ex(1, 3)
+        gt(0, 2)
+        mz(3, 3)
+        ex(3, 1)
+        zb(3, 0)
+        mv(0, 0)
+        ex(2, 1)
+        zb(3, 3)
+        mz(3, 2)
+        ex(3, 0)
+        gt(0, 0)
+        mv(0, 3)
+        ex(3, 3)
+        zb(3, 2)
+        mg(0, 1)
+        ex(2, 3)
+        gt(0, 3)
+        mg(1, 1)
+        ex(3, 2)
+        max_all()
+        qc(1, 0)
         tv(0, 1)
-        sums(1)
-        ec(2, 1, 0)
-        sc(2, 3)
-        sc(2, 1)
-        qc(2, 0)
-        tg(1, 1)
-        spread(0)
-        mg(1, 0)
-        pr(1)
-        bal(0, 2)
-        mv(1, 1)
-        sc(3, 0)
-        bal(0, 1)
-        sums(2)
-        pw2(1)
-        tg(1, 0)
-        bal(0, 3)
-        ev(0, 1)
-        bal(0, 0)
-        spread(1)
-        sc(3, 1)
-        gt(1, 1)
-        mv(1, 0)
-        pr(2)
-        bal(1, 1)
-        sums(3)
-        mass_order()
-        gt(1, 0)
-        pw2(2)
-        bal(1, 2)
+        tg(0, 1)
+        max_diff()
         mg(1, 2)
-        tg(2, 3)
-        bal(1, 3)
-        pr(3)
-        spread(2)
-        bal(1, 0)
-        mg(2, 1)
+        max_corr()
+        tg(1, 1)
+        first1()
+        mg(1, 0)
+        first2()
+        ev(0, 1)
+        first3()
+        first4()
+        mv(0, 1)
         tg(1, 2)
-        bal(2, 1)
-        pw2(3)
-        mg(3, 3)
-        tg(2, 1)
-        bal(2, 3)
+        sc(0, 3)
+        tc_(2, 1, 0)
+        sc(2, 1)
+        sc(3, 3)
+        gt(0, 1)
+        tc_(2, 1, 1)
+        sc(1, 0)
+        sc(1, 3)
+        tv(0, 0)
+        sc(1, 1)
+        tc_(2, 0, 0)
+        sc(1, 2)
+        sc(2, 0)
+        mv(1, 1)
+        sc(2, 2)
+        sc(0, 0)
+        sums(1)
+        ev(0, 0)
+        sc(3, 2)
+        gt(1, 1)
+        tg(1, 0)
+        sc(0, 2)
+        qv(0)
+        sc(0, 1)
         mv(1, 2)
-        tg(3, 3)
-        bal(2, 2)
+        sc(2, 3)
+        pw1(1)
+        sc(3, 1)
+        mv(1, 0)
+        gt(1, 2)
+        ec(2, 1, 1)
+        pw2(1)
+        sums(0)
+        gt(1, 0)
+        ec(2, 1, 0)
+        mass_order()
+        spread(1)
+        mg(1, 3)
+        pw1(0)
+        sc(3, 0)
+        bal(1, 1)
+        tv(1, 0)
+        pw2(0)
+        ec(2, 0, 0)
+        mg(2, 2)
+        bal(1, 3)
+        tg(1, 3)
+        sums(3)
+        qc(2, 0)
+        gm(1, 1)
+        ev(1, 0)
+        bal(1, 2)
+        tg(2, 2)
+        bal(1, 0)
+        spread(0)
+        mv(1, 3)
+        pw1(3)
+        gm(0, 1)
+        tc_(3, 0, 0)
+        bal(0, 2)
+        tc_(3, 1, 1)
+        bal(0, 0)
+        pw2(3)
+        ec(3, 0, 0)
+        tc_(3, 1, 0)
+        gt(1, 3)
+        ec(3, 1, 1)
+        sums(2)
+        bal(0, 1)
+        gm(0, 0)
+        ec(3, 1, 0)
+        bal(0, 3)
         spread(3)
+        qc(3, 0)
+        gm(1, 0)
+        mg(2, 1)
+        pw1(2)
+        bal(3, 2)
+        pw2(2)
+        mg(2, 3)
+        bal(3, 1)
+        tg(2, 1)
+        bal(3, 3)
+        gm(1, 3)
+        mg(3, 3)
+        tg(2, 3)
+        bal(3, 0)
+        spread(2)
+        tg(3, 3)
+        tv(1, 1)
+        gm(0, 3)
         tc_(3, 0, 1)
         bal(2, 0)
-        tc_(3, 1, 0)
-        bal(3, 3)
+        ev(1, 1)
+        tc_(2, 0, 1)
+        bal(2, 2)
         ec(3, 0, 1)
-        tc_(3, 1, 1)
-        bal(3, 1)
-        ec(3, 1, 0)
-        tc_(3, 0, 0)
-        ec(3, 1, 1)
-        bal(3, 2)
-        mv(2, 3)
-        ec(3, 0, 0)
-        bal(3, 0)
-        gt(1, 2)
-        mg(2, 2)
+        mg(2, 0)
+        gm(0, 2)
+        bal(2, 3)
+        ec(2, 0, 1)
+        mg(3, 0)
+        bal(2, 1)
+        tg(2, 0)
+        mg(3, 2)
+        qc(2, 1)
+        tg(3, 0)
+        gm(1, 2)
+        mg(3, 1)
         second1()
         qc(3, 1)
-        mg(3, 2)
-        second2()
-        qc(3, 0)
-        tg(2, 2)
-        tv(1, 0)
-        weigh(0, 1)
         tg(3, 2)
-        tv(0, 0)
-        mv(3, 3)
-        ev(1, 0)
+        mv(2, 0)
+        second2()
+        qv(1)
+        tg(3, 1)
+        mv(3, 0)
         weigh(3, 1)
-        mv(2, 2)
-        ev(0, 0)
+        ws(0, 0)
+        mv(2, 1)
+        gt(2, 0)
+        ws(0, 1)
+        tp(3, 1)
+        gt(2, 1)
+        tp(0, 0)
+        mv(3, 1)
+        gt(3, 0)
+        ep(3, 1)
         tp(0, 1)
         weigh(3, 0)
-        tv(1, 1)
-        tp(3, 1)
-        ep(0, 1)
-        ev(1, 1)
-        gt(2, 3)
-        tp(3, 0)
-        ep(3, 1)
-        gt(2, 2)
-        mg(3, 1)
-        ep(3, 0)
-        weigh(1, 0)
-        tv(2, 1)
-        tg(3, 1)
-        mv(2, 1)
-        weigh(1, 1)
-        tp(1, 0)
-        mv(3, 1)
-        qp(3, 0)
-        gt(3, 3)
-        tp(1, 1)
-        qp(3, 1)
-        mg(2, 0)
-        gt(2, 1)
-        ep(1, 0)
-        qv(0)
-        mg(3, 0)
-        ep(1, 1)
-        gt(3, 1)
-        tg(2, 0)
-        weigh(2, 1)
-        tg(3, 0)
+        ep(0, 0)
+        mv(2, 2)
+        ws(1, 1)
         mv(3, 2)
-        mv(2, 0)
-        ev(2, 1)
-        weigh(2, 0)
-        mv(3, 0)
-        tp(2, 1)
-        gt(2, 0)
-        tp(2, 0)
-        gt(3, 0)
-        tv(2, 0)
-        gt(3, 2)
+        gt(3, 1)
+        tp(3, 0)
+        gt(2, 2)
+        ep(0, 1)
         tv(3, 0)
-        ev(2, 0)
-        qv(1)
-        tv(3, 1)
-        weigh(0, 0)
+        gt(3, 2)
+        mv(2, 3)
+        ws(1, 0)
+        weigh(2, 1)
+        mv(3, 3)
+        ep(3, 0)
+        tv(2, 0)
+        gt(2, 3)
+        tp(1, 0)
         ev(3, 0)
+        tp(2, 1)
+        gt(3, 3)
+        ev(2, 0)
+        tv(2, 1)
+        qp(3, 0)
+        tp(1, 1)
+        weigh(2, 0)
+        ev(2, 1)
+        tv(3, 1)
         my(3, 0)
         ev(3, 1)
+        qp(3, 1)
         qv(2)
-        tp(0, 0)
-        qv(3)
-        ep(2, 0)
-        qp(1)
         ep(2, 1)
+        tp(2, 0)
+        qv(3)
+        ep(1, 0)
+        qp(0)
+        ep(1, 1)
         my(3, 1)
-        ep(0, 0)
+        ep(2, 0)
+        my(0)
+        qp(1)
+        fin(3)
         my(1)
         qp(2)
-        qp(0)
-        my(2)
-        fin(3)
-        fin(1)
-        my(0)
-        fin(2)
         fin(0)
+        my(2)
+        fin(1)
+        fin(2)

from contextlib import ExitStack
from math import sqrt

import concourse.mybir as mybir
from concourse.masks import make_identity

T, S, D, C, F = 2048, 512, 1024, 1024, 512
TAU = 0.75
FLOPS = 2 * (S * T * D + T * D * F + T * C * F + S * T * F)

F32 = mybir.dt.float32
BF16 = mybir.dt.bfloat16
U32 = mybir.dt.uint32
U8 = mybir.dt.uint8
F8 = mybir.dt.float8_e4m3fn
FP8X4 = mybir.dt.float8_e4m3fn_x4
ALU = mybir.AluOpType
ACT = mybir.ActivationFunctionType
AX = mybir.AxisListType

P = 128
CH = 4
NT = 512
ST = 4
FT = 4
KP = 2
GB = 4
TR = 5
GS = 2
CB = 4


def tile_sinkhorn_slot_mixing_f5_kernel(
    tc, a_bytes, a_scale, c, e, wg, wv, beta, mass, bg, bo, out
):
    nc = tc.nc
    with ExitStack() as ctx:
        keep = ctx.enter_context(tc.tile_pool(name="keep", bufs=1))
        work = ctx.enter_context(tc.tile_pool(name="work", bufs=2))
        psum = ctx.enter_context(tc.psum_pool(name="psum", bufs=4))

        ident = keep.tile([P, P], F32, name="ident")
        make_identity(nc, ident[:])
        ident16 = keep.tile([P, P], BF16, name="ident16")
        make_identity(nc, ident16[:])

        scale = keep.tile([P, D], F32, name="scale")
        ab = [keep.tile([P, 4, D], U8, name="ab%d" % i) for i in range(CH)]
        vec = keep.tile([P, P], BF16, name="vec")
        mass_n = keep.tile([P, T], BF16, name="mass_n")
        mass_p = keep.tile([P, T], BF16, name="mass_p")
        bo_b = keep.tile([P, F], BF16, name="bo_b")
        a_codes = [keep.tile([P, KP, NT], U32, name="a_codes%d" % i, align_bytes=64) for i in range(CH)]
        a_planes = [keep.tile([P, KP, NT], U8, name="a_planes%d" % i, align_bytes=64) for i in range(CH)]
        e_codes = keep.tile([P, KP, S], U32, name="e_codes", align_bytes=64)
        e_planes = keep.tile([P, KP, S], U8, name="e_planes", align_bytes=64)
        wg_codes = keep.tile([P, KP, F], U32, name="wg_codes", align_bytes=64)
        wg_planes = keep.tile([P, KP, F], U8, name="wg_planes", align_bytes=64)
        wv_codes = keep.tile([P, KP, F], U32, name="wv_codes", align_bytes=64)
        wv_planes = keep.tile([P, KP, F], U8, name="wv_planes", align_bytes=64)
        v_codes = [keep.tile([P, F], U32, name="v_codes%d" % i, align_bytes=64) for i in range(CH)]
        v_planes = [keep.tile([P, F], U8, name="v_planes%d" % i, align_bytes=64) for i in range(CH)]
        ew = keep.tile([P, ST, T], F32, name="ew")
        nbeta = keep.tile([P, ST], F32, name="nbeta")
        bgh = keep.tile([P, FT], F32, name="bgh")
        nm = keep.tile([P, ST, CH], F32, name="nm")
        s_acc = keep.tile([P, ST, CH], F32, name="s_acc")
        q_acc = keep.tile([P, ST, CH], F32, name="q_acc")
        expo = keep.tile([P, 4], F32, name="expo")
        dummy = keep.tile([P, 1], F32, name="dummy")
        junk = keep.tile([P, P], F32, name="junk")

        a_view = a_bytes.rearrange("(c m t) d -> c m t d", c=CH, m=P, t=4)
        c_view = c.rearrange("(c m t) d -> c m t d", c=CH, m=P, t=4)

        nc.vector.memset(vec[:], 0.0)
        nc.vector.memset(dummy[:], 0.0)
        nc.gpsimd.memset(expo[:], -TAU)

        x = {}
        grouped = {}
        gated = {}
        th = {}
        c_raw = {}
        w_raw = {}
        banks = {}
        codes = {}
        pt = {}
        pcodes = {}
        cr = {}
        raw = {}
        small = {}
        w_codes = {"wg": (wg_codes, wg_planes), "wv": (wv_codes, wv_planes)}

        def bank(key, tag):
            banks[key] = psum.tile([P, 512], F32, name="bank_" + tag, tag=tag, bufs=TR if tag == "tr" else 8 - TR)
            return banks[key]

        def group(key):
            if key not in grouped:
                grouped[key] = work.tile([P, 2048], BF16, name="grouped", tag="grouped", bufs=GB, align_bytes=64)
            return grouped[key]

        def turn(key, i, words):
            b = bank((key, i), "tr")
            for j in range(4):
                nc.tensor.transpose(b[:, P * j : P * (j + 1)], words(j // 2, j % 2), ident[:])

        def weave(key, i, dst, h, pattern):
            nc.scalar.copy(
                out=group(dst)[:].bitcast(F32)[:, 512 * h : 512 * (h + 1)].rearrange("p (a r u) -> p a r u", a=2, u=2) if pattern == 0
                else group(dst)[:].bitcast(F32)[:, 512 * h : 512 * (h + 1)].rearrange("p (r a u) -> p r a u", a=2, u=2),
                in_=banks[key, i][:].rearrange("p (a u r) -> p a r u", a=2, u=2) if pattern == 0
                else banks[key, i][:].rearrange("p (a u r) -> p r a u", a=2, u=2),
            )

        def load_scale(g):
            cols = slice(512 * g, 512 * (g + 1))
            nc.scalar.dma_start(out=scale[:, cols], in_=a_scale[:, cols].rearrange("o k -> (o k)").partition_broadcast(P))

        def load_e():
            raw["e"] = work.tile([P, ST, D], BF16, name="e_raw", tag="raw", bufs=4)
            nc.sync.dma_start(out=raw["e"][:], in_=e.rearrange("(s p) d -> p s d", p=P))

        def load_c(i):
            c_raw[i] = work.tile([P, 4, C], BF16, name="c_raw", tag="raw", bufs=4)
            nc.sync.dma_start(out=c_raw[i][:], in_=c_view[i])

        def load_w(key, w):
            w_raw[key] = work.tile([P, KP, 4, F], BF16, name="w_raw", tag="raw", bufs=4)
            nc.sync.dma_start(out=w_raw[key][:], in_=w.rearrange("(g p j) f -> p g j f", p=P, j=4))

        def prod(i, t, g=None):
            cols = slice(0, D) if g is None else slice(D // 2 * g, D // 2 * (g + 1))
            if (i, t) not in x:
                x[i, t] = work.tile([P, D], BF16, name="x", tag="x", bufs=5)
            nc.vector.tensor_tensor(out=x[i, t][:, cols], in0=ab[i][:, t, cols].bitcast(F8), in1=scale[:, cols], op=ALU.mult)

        def step2(words, g, u):
            return words[:, 256 * g + u : 256 * (g + 1) : 2]

        def ta(i, h, g):
            turn("a", (i, h, g), lambda a, u: step2(x[i, 2 * h + a][:].bitcast(F32), g, u))

        def ea(i, h, g):
            weave("a", (i, h, g), ("a", i, g), h, 1)

        def tc_(i, h, g):
            turn("c", (i, h, g), lambda a, u: step2(c_raw[i][:, 2 * h + a, :].bitcast(F32), g, u))

        def ec(i, h, g):
            weave("c", (i, h, g), ("c", i, g), h, 1)

        def te(g, h):
            turn("e", (g, h), lambda a, u: step2(raw["e"][:, 2 * h + a, :].bitcast(F32), g, u))

        def ee(g, h):
            weave("e", (g, h), ("e", g), h, 0)

        def tv(i, h):
            turn("tv", (i, h), lambda a, u: gated[i][:, 2 * h + a, :].bitcast(F32)[:, P * u : P * (u + 1)])

        def ev(i, h):
            weave("tv", (i, h), ("v", i), h, 0)

        def tp(s, h):
            turn("tp", (s, h), lambda a, u: pt[s][:].bitcast(F32)[:, 256 * (2 * h + a) + P * u : 256 * (2 * h + a) + P * (u + 1)])

        def ep(s, h):
            weave("tp", (s, h), ("p", s), h, 0)

        def ww(key, g, h):
            nc.scalar.copy(
                out=group((key, g))[:, 1024 * h : 1024 * (h + 1)].rearrange("p (c i j) -> p c j i", i=4, j=4),
                in_=w_raw[key][:, g, :, 256 * h : 256 * (h + 1)].rearrange("p j (c i) -> p c j i", i=4),
            )

        def quant(dst, plane, key):
            nc.vector.quantize_mx(out=dst.bitcast(FP8X4), scales=plane, in_=grouped[key][:])

        def qa(i, g):
            quant(a_codes[i][:, g, :], a_planes[i][:, g, :], ("a", i, g))

        def qc(i, g):
            cc = work.tile([P, NT], U32, name="c_codes", tag="c_codes", bufs=CB, align_bytes=64)
            cp = work.tile([P, NT], U8, name="c_planes", tag="c_planes", bufs=CB, align_bytes=64)
            codes["c", i, g] = (cc, cp)
            quant(cc[:], cp[:], ("c", i, g))

        def qe(g):
            quant(e_codes[:, g, :], e_planes[:, g, :], ("e", g))

        def qw(key, g):
            quant(w_codes[key][0][:, g, :], w_codes[key][1][:, g, :], (key, g))

        def qv(i):
            quant(v_codes[i][:], v_planes[i][:], ("v", i))

        def qp(s, h=None):
            if s not in pcodes:
                pc = work.tile([P, CH * P], U32, name="p_codes", tag="p_codes", bufs=4, align_bytes=64)
                pp = work.tile([P, CH * P], U8, name="p_planes", tag="p_planes", bufs=4, align_bytes=64)
                pcodes[s] = (pc, pp)
            pc, pp = pcodes[s]
            cols = slice(0, 512) if h is None else slice(256 * h, 256 * (h + 1))
            nc.vector.quantize_mx(
                out=pc[:, cols].bitcast(FP8X4), scales=pp[:, cols], in_=grouped["p", s][:, 4 * cols.start : 4 * cols.stop]
            )

        def mm(b, lhs, lhs_p, rhs, rhs_p, first, last):
            nc.tensor.matmul_mx(out=b[:], lhsT=lhs.bitcast(FP8X4), lhsT_scale=lhs_p, rhs=rhs.bitcast(FP8X4), rhs_scale=rhs_p, start=first, stop=last)

        def mz(i, s):
            b = bank(("z", i, s), "mm")
            for g in range(KP):
                mm(b, e_codes[:, g, P * s : P * (s + 1)], e_planes[:, g, P * s : P * (s + 1)], a_codes[i][:, g, :], a_planes[i][:, g, :], g == 0, g == 1)

        def mg(i, f):
            b = bank(("g", i, f), "mm")
            for g in range(KP):
                mm(b, wg_codes[:, g, P * f : P * (f + 1)], wg_planes[:, g, P * f : P * (f + 1)], a_codes[i][:, g, :], a_planes[i][:, g, :], g == 0, g == 1)

        def mv(i, f):
            b = bank(("v", i, f), "mm")
            for g in range(KP):
                mm(b, wv_codes[:, g, P * f : P * (f + 1)], wv_planes[:, g, P * f : P * (f + 1)], codes["c", i, g][0][:], codes["c", i, g][1][:], g == 0, g == 1)

        def chunk(i):
            return slice(NT * i, NT * (i + 1))

        def zb(i, s):
            nc.vector.tensor_scalar(
                out=ew[:, s, chunk(i)], in0=banks["z", i, s][:], scalar1=nbeta[:, s : s + 1], scalar2=3.0e38,
                op0=ALU.mult, op1=ALU.min, accum_out=nm[:, s, i : i + 1],
            )

        def ex(i, s):
            nc.scalar.activation(
                out=ew[:, s, chunk(i)], in_=ew[:, s, chunk(i)], func=ACT.Exp, bias=nm[:, s, i : i + 1], scale=-1.0,
                accum_out=s_acc[:, s, i : i + 1],
            )

        def tg(i, f):
            if i not in th:
                th[i] = work.tile([P, FT, NT], F32, name="th", tag="th", bufs=3)
            nc.scalar.activation(out=th[i][:, f, :], in_=banks["g", i, f][:], func=ACT.Tanh, bias=bgh[:, f : f + 1], scale=0.5)

        def gt(i, f):
            if i not in gated:
                gated[i] = work.tile([P, FT, NT], BF16, name="gated", tag="gated", bufs=2)
            nc.vector.scalar_tensor_tensor(
                out=gated[i][:, f, :], in0=th[i][:, f, :], scalar=1.0, in1=banks["v", i, f][:], op0=ALU.add, op1=ALU.mult
            )

        def vec_t():
            banks["vec"] = psum.tile([P, 1024], BF16, name="bank_vec", tag="tr", bufs=TR)
            nc.tensor.transpose(banks["vec"][:, 0:P], vec[:], ident16[:])

        def vec_bg():
            nc.vector.tensor_scalar(out=bgh[:], in0=banks["vec"][:, 0:4], scalar1=0.5, scalar2=None, op0=ALU.mult)

        def vec_beta():
            nc.vector.tensor_scalar(out=nbeta[:], in0=banks["vec"][:, 4:8], scalar1=-1.0, scalar2=None, op0=ALU.mult)

        def mass_order():
            nc.scalar.copy(
                out=mass_p[:].bitcast(F32).rearrange("q (c u p) -> q c u p", c=CH, u=2),
                in_=mass_n[:].bitcast(F32).rearrange("q (c p u) -> q c u p", c=CH, u=2),
            )

        def wide(t):
            return t[:].unsqueeze(2).to_broadcast([P, ST, CH])

        def stat(name, shape):
            small[name] = keep.tile(shape, F32, name=name)
            return small[name]

        def max_all():
            nc.vector.tensor_reduce(out=stat("nmin", [P, ST])[:], in_=nm[:], axis=AX.X, op=ALU.min)

        def max_diff():
            nc.vector.tensor_tensor(out=stat("d", [P, ST, CH])[:], in0=wide(small["nmin"]), in1=nm[:], op=ALU.subtract)

        def max_corr():
            nc.scalar.activation(out=stat("corr", [P, ST, CH])[:], in_=small["d"][:], func=ACT.Exp)

        def first1():
            nc.vector.tensor_tensor(out=stat("f_prod", [P, ST, CH])[:], in0=small["corr"][:], in1=s_acc[:], op=ALU.mult)

        def first2():
            nc.vector.tensor_reduce(out=stat("f_sum", [P, ST])[:], in_=small["f_prod"][:], axis=AX.X, op=ALU.add)

        def first3():
            nc.vector.reciprocal(out=stat("f_rec", [P, ST])[:], in_=small["f_sum"][:])

        def first4():
            nc.vector.tensor_tensor(out=stat("first", [P, ST, CH])[:], in0=small["corr"][:], in1=wide(small["f_rec"]), op=ALU.mult)

        def second1():
            nc.vector.tensor_reduce(out=stat("s_sum", [P, ST])[:], in_=q_acc[:], axis=AX.X, op=ALU.add)

        def second2():
            nc.vector.reciprocal(out=stat("second", [P, ST])[:], in_=small["s_sum"][:])

        def sc(i, s):
            if s >= GS:
                nc.gpsimd.tensor_scalar(
                    out=ew[:, s, chunk(i)], in0=ew[:, s, chunk(i)], scalar1=small["first"][:, s, i : i + 1], scalar2=1.0e-37,
                    op0=ALU.mult, op1=ALU.add,
                )
                return
            nc.scalar.activation(
                out=ew[:, s, chunk(i)], in_=ew[:, s, chunk(i)], func=ACT.Copy, bias=1.0e-37, scale=small["first"][:, s, i : i + 1]
            )

        def sums(i):
            b = bank(("r", i), "tr")
            for k in range(4):
                for s in range(ST):
                    nc.tensor.matmul(
                        b[:, P * k : P * (k + 1)], lhsT=ew[:, s, NT * i + P * k : NT * i + P * (k + 1)], rhs=ident[:],
                        start=(s == 0), stop=(s == ST - 1), is_transpose=True,
                    )

        def pw1(i):
            nc.vector.tensor_reduce(out=stat("rc%d" % i, [P, 4])[:], in_=banks["r", i][:].rearrange("p (k r) -> p k r", k=4), axis=AX.X, op=ALU.add)

        def pr(i):
            rc = stat("rc%d" % i, [P, 4])
            for k in range(4):
                nc.scalar.activation(
                    out=junk[:], in_=banks["r", i][:, P * k : P * (k + 1)], func=ACT.Copy, accum_out=rc[:, k : k + 1]
                )

        def pw2(i):
            nc.gpsimd.tensor_tensor(out=stat("wt%d" % i, [P, 4])[:], in0=small["rc%d" % i][:], in1=expo[:], op=ALU.pow)

        def spread(i):
            b = bank(("w", i), "tr")
            for k in range(4):
                nc.tensor.transpose(b[:, P * k : P * (k + 1)], small["wt%d" % i][:, k : k + 1].to_broadcast([P, P]), ident[:])

        def bal(i, s):
            nc.vector.scalar_tensor_tensor(
                out=ew[:, s, chunk(i)], in0=ew[:, s, chunk(i)], scalar=1.0, in1=banks["w", i][:], op0=ALU.mult, op1=ALU.mult,
                accum_out=q_acc[:, s, i : i + 1],
            )

        def weigh(s, h):
            if s not in pt:
                pt[s] = work.tile([P, T], BF16, name="pt", tag="pt", bufs=2)
            half = slice(T // 2 * h, T // 2 * (h + 1))
            nc.vector.scalar_tensor_tensor(
                out=pt[s][:, half], in0=ew[:, s, half], scalar=small["second"][:, s : s + 1], in1=mass_p[:, half],
                op0=ALU.mult, op1=ALU.mult,
            )

        def gm(s, i):
            nc.gpsimd.tensor_tensor(out=ew[:, s, chunk(i)], in0=ew[:, s, chunk(i)], in1=mass_p[:, chunk(i)], op=ALU.mult)

        def ws(s, h):
            if s not in pt:
                pt[s] = work.tile([P, T], BF16, name="pt", tag="pt", bufs=2)
            half = slice(T // 2 * h, T // 2 * (h + 1))
            nc.scalar.activation(out=pt[s][:, half], in_=ew[:, s, half], func=ACT.Copy, scale=small["second"][:, s : s + 1])

        def my(s, h=None):
            if ("y", s) not in banks:
                bank(("y", s), "mm")
            b = banks["y", s]
            pc, pp = pcodes[s]
            for i in range(CH) if h is None else (2 * h, 2 * h + 1):
                cols = slice(P * i, P * (i + 1))
                mm(b, pc[:, cols], pp[:, cols], v_codes[i][:], v_planes[i][:], i == 0, i == CH - 1)

        def fin(s):
            y = work.tile([P, F], F32, name="y", tag="y", bufs=4)
            nc.vector.scalar_tensor_tensor(out=y[:], in0=banks["y", s][:], scalar=0.5 * sqrt(T), in1=bo_b[:], op0=ALU.mult, op1=ALU.add)
            nc.sync.dma_start(out=out[P * s : P * (s + 1), :], in_=y[:])

        ctx.enter_context(tc.manual_schedule())

        nc.sync.dma_start(out=ab[0][:, 0:2, :], in_=a_view[0][:, 0:2, :])
        load_scale(0)
        nc.sync.dma_start(out=ab[0][:, 2:4, :], in_=a_view[0][:, 2:4, :])
        load_scale(1)
        nc.scalar.dma_start(out=vec[0:4, :], in_=bg.rearrange("(r f) -> r f", f=P))
        nc.scalar.dma_start(out=vec[4:8, :], in_=beta.rearrange("(r f) -> r f", f=P))
        nc.scalar.activation(out=dummy[:], in_=dummy[:], func=ACT.Exp)
        nc.sync.dma_start(out=ab[1][:], in_=a_view[1])
        load_e()
        load_w("wg", wg)
        nc.sync.dma_start(out=ab[2][:], in_=a_view[2])
        nc.sync.dma_start(out=ab[3][:], in_=a_view[3])

        load_w("wv", wv)
        load_c(0)
        prod(0, 0, 0)
        prod(0, 3, 0)
        prod(0, 1, 0)
        vec_t()
        prod(0, 2, 0)
        ta(0, 0, 0)
        prod(0, 3, 1)
        ta(0, 1, 0)
        prod(0, 0, 1)
        ea(0, 0, 0)
        prod(0, 2, 1)
        ea(0, 1, 0)
        prod(0, 1, 1)
        ta(0, 1, 1)
        vec_beta()
        prod(1, 3)
        ta(0, 0, 1)
        ea(0, 1, 1)
        te(0, 1)
        prod(1, 1)
        ea(0, 0, 1)
        te(1, 0)
        ee(0, 1)
        te(1, 1)
        qa(0, 1)
        ee(1, 0)
        te(0, 0)
        prod(1, 0)
        ww("wg", 0, 1)
        load_c(1)
        nc.sync.dma_start(out=mass_n[:], in_=mass.partition_broadcast(P))
        nc.sync.dma_start(out=bo_b[:], in_=bo.partition_broadcast(P))
        prod(1, 2)
        ee(0, 0)
        ta(1, 0, 1)
        ee(1, 1)
        ta(1, 0, 0)
        qe(0)
        ww("wg", 0, 0)
        ta(1, 1, 1)
        qe(1)
        ta(1, 1, 0)
        qa(0, 0)
        ea(1, 0, 1)
        qw("wg", 0)
        ea(1, 1, 0)
        mz(0, 0)
        prod(2, 1)
        ww("wv", 0, 1)
        mz(0, 1)
        prod(2, 3)
        ww("wv", 1, 1)
        mz(0, 2)
        zb(0, 0)
        ww("wv", 0, 0)
        tc_(0, 1, 0)
        prod(2, 2)
        tc_(0, 1, 1)
        ea(1, 1, 1)
        mz(0, 3)
        zb(0, 2)
        ea(1, 0, 0)
        ta(2, 1, 0)
        qa(1, 1)
        ex(0, 0)
        tc_(1, 1, 1)
        zb(0, 3)
        ex(0, 2)
        qw("wv", 0)
        ww("wv", 1, 0)
        qa(1, 0)
        ec(0, 1, 0)
        vec_bg()
        prod(3, 0)
        mz(1, 0)
        load_c(2)
        ec(0, 1, 1)
        ex(0, 3)
        qw("wv", 1)
        tc_(1, 0, 0)
        ea(2, 1, 0)
        prod(2, 0)
        mz(1, 1)
        ww("wg", 1, 1)
        ta(2, 1, 1)
        zb(1, 0)
        ta(2, 0, 0)
        ww("wg", 1, 0)
        zb(0, 1)
        ta(2, 0, 1)
        prod(3, 1)
        mz(1, 3)
        ex(0, 1)
        load_c(3)
        ea(2, 0, 0)
        mz(1, 2)
        qw("wg", 1)
        ex(1, 0)
        zb(1, 3)
        tc_(0, 0, 1)
        ea(2, 0, 1)
        qa(2, 0)
        mg(0, 3)
        ea(2, 1, 1)
        zb(1, 2)
        ta(3, 0, 1)
        ec(1, 0, 0)
        qa(2, 1)
        mg(0, 2)
        tg(0, 3)
        prod(3, 2)
        ea(3, 0, 1)
        tc_(0, 0, 0)
        tg(0, 2)
        mz(2, 2)
        prod(3, 3)
        ex(1, 2)
        mz(2, 3)
        ec(0, 0, 0)
        zb(2, 2)
        ta(3, 0, 0)
        ec(0, 0, 1)
        qc(0, 0)
        ta(3, 1, 0)
        ex(2, 2)
        zb(2, 3)
        ta(3, 1, 1)
        ea(3, 0, 0)
        mz(2, 0)
        qc(0, 1)
        ea(3, 1, 0)
        zb(1, 1)
        mg(0, 0)
        ea(3, 1, 1)
        tc_(1, 0, 1)
        qa(3, 0)
        ec(1, 1, 1)
        qa(3, 1)
        mz(2, 1)
        ex(1, 1)
        zb(2, 0)
        tc_(1, 1, 0)
        tg(0, 0)
        zb(2, 1)
        ec(1, 0, 1)
        mz(3, 1)
        ex(2, 0)
        mv(0, 2)
        qc(1, 1)
        ec(1, 1, 0)
        mz(3, 0)
        zb(3, 1)
        ex(1, 3)
        gt(0, 2)
        mz(3, 3)
        ex(3, 1)
        zb(3, 0)
        mv(0, 0)
        ex(2, 1)
        zb(3, 3)
        mz(3, 2)
        ex(3, 0)
        gt(0, 0)
        mv(0, 3)
        ex(3, 3)
        zb(3, 2)
        mg(0, 1)
        ex(2, 3)
        gt(0, 3)
        mg(1, 1)
        ex(3, 2)
        max_all()
        qc(1, 0)
        tv(0, 1)
        tg(0, 1)
        max_diff()
        mg(1, 2)
        max_corr()
        tg(1, 1)
        first1()
        mg(1, 0)
        first2()
        ev(0, 1)
        first3()
        first4()
        mv(0, 1)
        tg(1, 2)
        sc(0, 3)
        tc_(2, 1, 0)
        sc(2, 1)
        sc(3, 3)
        gt(0, 1)
        tc_(2, 1, 1)
        sc(1, 0)
        sc(1, 3)
        tv(0, 0)
        sc(1, 1)
        tc_(2, 0, 0)
        sc(1, 2)
        sc(2, 0)
        mv(1, 1)
        sc(2, 2)
        sc(0, 0)
        sums(1)
        ev(0, 0)
        sc(3, 2)
        gt(1, 1)
        tg(1, 0)
        sc(0, 2)
        qv(0)
        sc(0, 1)
        mv(1, 2)
        sc(2, 3)
        pw1(1)
        sc(3, 1)
        mv(1, 0)
        gt(1, 2)
        ec(2, 1, 1)
        pw2(1)
        sums(0)
        gt(1, 0)
        ec(2, 1, 0)
        mass_order()
        spread(1)
        mg(1, 3)
        pw1(0)
        sc(3, 0)
        bal(1, 1)
        tv(1, 0)
        pw2(0)
        ec(2, 0, 0)
        mg(2, 2)
        bal(1, 3)
        tg(1, 3)
        sums(3)
        qc(2, 0)
        gm(1, 1)
        ev(1, 0)
        bal(1, 2)
        tg(2, 2)
        bal(1, 0)
        spread(0)
        mv(1, 3)
        pw1(3)
        gm(0, 1)
        tc_(3, 0, 0)
        bal(0, 2)
        tc_(3, 1, 1)
        bal(0, 0)
        pw2(3)
        ec(3, 0, 0)
        tc_(3, 1, 0)
        gt(1, 3)
        ec(3, 1, 1)
        sums(2)
        bal(0, 1)
        gm(0, 0)
        ec(3, 1, 0)
        bal(0, 3)
        spread(3)
        qc(3, 0)
        gm(1, 0)
        mg(2, 1)
        pw1(2)
        bal(3, 2)
        pw2(2)
        mg(2, 3)
        bal(3, 1)
        tg(2, 1)
        bal(3, 3)
        gm(1, 3)
        mg(3, 3)
        tg(2, 3)
        bal(3, 0)
        spread(2)
        tg(3, 3)
        tv(1, 1)
        gm(0, 3)
        tc_(3, 0, 1)
        bal(2, 0)
        ev(1, 1)
        tc_(2, 0, 1)
        bal(2, 2)
        ec(3, 0, 1)
        mg(2, 0)
        gm(0, 2)
        bal(2, 3)
        ec(2, 0, 1)
        mg(3, 0)
        bal(2, 1)
        tg(2, 0)
        mg(3, 2)
        qc(2, 1)
        tg(3, 0)
        gm(1, 2)
        mg(3, 1)
        second1()
        qc(3, 1)
        tg(3, 2)
        mv(2, 0)
        second2()
        qv(1)
        tg(3, 1)
        mv(3, 0)
        weigh(3, 1)
        ws(0, 0)
        mv(2, 1)
        gt(2, 0)
        ws(0, 1)
        tp(3, 1)
        gt(2, 1)
        tp(0, 0)
        mv(3, 1)
        gt(3, 0)
        ep(3, 1)
        tp(0, 1)
        weigh(3, 0)
        ep(0, 0)
        mv(2, 2)
        ws(1, 1)
        mv(3, 2)
        gt(3, 1)
        tp(3, 0)
        gt(2, 2)
        ep(0, 1)
        tv(3, 0)
        gt(3, 2)
        mv(2, 3)
        ws(1, 0)
        weigh(2, 1)
        mv(3, 3)
        ep(3, 0)
        tv(2, 0)
        gt(2, 3)
        tp(1, 0)
        ev(3, 0)
        tp(2, 1)
        gt(3, 3)
        ev(2, 0)
        tv(2, 1)
        qp(3, 0)
        tp(1, 1)
        weigh(2, 0)
        ev(2, 1)
        tv(3, 1)
        my(3, 0)
        ev(3, 1)
        qp(3, 1)
        qv(2)
        ep(2, 1)
        tp(2, 0)
        qv(3)
        ep(1, 0)
        qp(0)
        ep(1, 1)
        my(3, 1)
        ep(2, 0)
        my(0)
        qp(1)
        fin(3)
        my(1)
        qp(2)
        fin(0)
        my(2)
        fin(1)
        fin(2)
